import numpy as np, ml_dtypes
CORES = [9,25,41,57]
N = 4
BF = ml_dtypes.bfloat16
def gentries(a):
    return np.ascontiguousarray(a.reshape(8, 16, -1).transpose(0, 2, 1)).reshape(8, -1)
def gtable(e):
    e = np.asarray(e); return np.ascontiguousarray(e.reshape(8, -1, 16).transpose(0, 2, 1)).reshape(128, -1).astype(np.int32)
W0, B, LN, RO, SP, CAP = 3328, 256, 2048, 3, 3, 512
W = W0 + RO * B
def parts(rng):
    scale = np.array([0.5, 1, 1.5, 2, 3, 4, 6, 8])[np.argsort(rng.random((N, 8)), axis=1)][:, :, None, None]; dens = 0.1 + 0.6 * rng.random((N, 8, 1, W0))
    cnt = np.where(rng.random((N, 8, 16, W0)) < dens, np.minimum(15, 1 + (scale * rng.standard_exponential((N, 8, 16, W0))).astype(np.int64)), 0)
    hot = rng.integers(0, W0, (N, 8, 64))
    def some(n, share):
        return np.where(rng.random((N, 8, n)) < share, np.take_along_axis(hot, rng.integers(0, 64, (N, 8, n)), 2), rng.integers(0, W0, (N, 8, n)))
    ptr = some(16 * W0, 0.4).reshape(N, 8, 16, W0); suf = (np.arange(W0) * rng.random((N, 8, W0))).astype(np.int64)
    return cnt, ptr, suf, rng.integers(0, W0, (N, 8, W0)), some(LN, 0.3), rng.integers(0, 256, (N, 8, RO * SP, LN))
def levels(rng, cnt, suf, v, g):
    x = np.arange(W0); b = np.where(x <= 16, 3, np.where(x <= 32, 2, np.where(x <= 48, 1, 0)))
    cnt[:, g] = np.where((np.arange(16) >> 2)[:, None] == b, rng.integers(1, 16, (N, 16, W0)), 0)
    suf[:, g] = rng.integers(1, 17, (N, W0)) + 16 * np.maximum(2 - b, 0)
    v[:, g, :SP - 1, :B] = rng.integers(240, 256, (N, SP - 1, B)); v[:, g, SP - 1, :B] = rng.integers(0, 128, (N, B))
def clones(rng, cnt, ptr, suf, lnk, cx, v, g):
    o = 1 + np.argsort(rng.random((N, W0 - 1)), axis=1); x = o[:, :B]; b = o[:, B:2 * B]; u = o[:, 2 * B:3 * B]
    qi = np.arange(N)[:, None]; z = rng.integers(1, 16, (N, B)); ct = cnt[:, g]; pt = ptr[:, g]
    for y in (x, u):
        ct[qi, :, y] = 0; ct[qi, 0, y] = 1; pt[qi, 0, y] = y
    ct[qi, :, b] = 0; ct[qi, z, b] = 1; pt[qi, z, b] = u
    suf[qi, g, x] = b; suf[qi, g, u] = x; lnk[qi, g, u] = np.maximum(lnk[qi, g, u], 1); cx[:, g, :B] = x
    v[:, g, :, :B] = rng.integers(0, 64, (N, RO * SP, B))
    for s in (SP - 2, 2 * SP - 2): v[:, g, s, :B] = rng.integers(128, 256, (N, B))
    if (RO - 2) * SP > 2:
        v[:, g, RO * SP - 2, :B] = rng.integers(64, 128, (N, B)); v[:, g, RO * SP - 1, :B] = rng.integers(128, 256, (N, B))
def kept(rng, cnt, ptr, suf, cx, v, g):
    o = 1 + np.argsort(rng.random((N, W0 - 1)), axis=1)[:, :(SP + 1) * B]; h = o[:, :SP * B]; b = o[:, SP * B:]
    qi = np.arange(N)[:, None]; z = rng.integers(1, 16, (N, B)); ct = cnt[:, g]; pt = ptr[:, g]
    ct[qi, :, h] = 0; ct[qi, 0, h] = 1; pt[qi, 0, h] = h; suf[qi, g, h] = o[:, B:]
    ct[qi, :, b] = 0; ct[qi, z, b] = 1; cx[:, g] = o[:, np.arange(LN) % B]
    v[:, g, :SP] = rng.integers(0, 128, (N, SP, LN)); v[1::2, g, SP - 1, :B] = rng.integers(128, 256, (N // 2, B))
    v[:, g, 2 * SP - 1, :B] = rng.integers(0, 128, (N, B))
def filled(rng, cnt, ptr, suf, lnk, cx, v, g):
    o = 1 + np.argsort(rng.random((N, W0 - 1)), axis=1)[:, :(2 * SP + 1) * B]; x = o[:, :B]; y = o[:, B:]; b1 = o[:, SP * B:(SP + 1) * B]; b2 = o[:, 2 * SP * B:]
    qi = np.arange(N)[:, None]; ct = cnt[:, g]; pt = ptr[:, g]
    ct[qi, :, o] = 0; ct[qi, 0, o] = 1; pt[qi, 0, o] = o
    for b, lo in ((b1, 1), (b2, 8)):
        ct[qi, 0, b] = 0; ct[qi, rng.integers(lo, lo + 7, (N, B)), b] = 1
    suf[qi, g, x] = np.roll(x, -1, axis=1); suf[qi, g, y[:, :-B]] = y[:, B:]; lnk[qi, g, x] = np.roll(y[:, :B], -1, axis=0)
    cx[:, g] = x[:, np.arange(LN) % B]
    v[:, g, :2 * SP] = rng.integers(0, 128, (N, 2 * SP, LN)); v[:, g, SP - 1, :B] = rng.integers(128, 256, (N, B))
    q4 = np.arange(N) % 4; v[:, g, 2 * SP - 1, :B // 2] += 128 * ((q4 == 1) | (q4 == 2))[:, None]
    if RO > 2: v[:, g, 3 * SP - 1, :B // 2] = rng.integers(0, 128, (N, B // 2))
def pack(cnt, ptr, suf, lnk, cx, v):
    return {"tab": np.ascontiguousarray((16 * ptr + cnt).reshape(N, 128, W0)).astype(np.int32), "suf": suf.astype(np.int32), "lnk": lnk.astype(np.int32),
            "cx": np.stack([gtable(a) for a in cx]), "vv": v.reshape(N, 8, RO * SP * LN).astype(np.float32).astype(BF)}
def setup_inputs(rng):
    return pack(*parts(rng))
def setup_inputs_room(rng):
    cnt, ptr, suf, lnk, cx, v = parts(rng)
    cnt = np.where(np.arange(16)[:, None] == rng.integers(0, 16, (N, 8, 1, W0)), np.maximum(cnt, 1), cnt); ptr = np.maximum(ptr, 1); cx = np.maximum(cx, 1)
    v[:, :, :SP - 1] = rng.integers(0, 128, (N, 8, SP - 1, LN)); opts = (0, 1, CAP - 1, CAP, CAP + 1, LN)
    for q in range(N):
        o = rng.permutation(6)
        for g in range(6):
            m = opts[g] if q == 0 else opts[5 - g] if q == 1 else opts[int(o[g])]
            v[q, g, SP - 1] = np.where(rng.permutation(LN) < m, rng.integers(240, 256, LN), rng.integers(0, 128, LN))
    for g in (6, 7):
        levels(rng, cnt, suf, v, g)
        for q in range(N): cx[q, g, :B] = 64 + rng.permutation(W0 - 64)[:B]
    return pack(cnt, ptr, suf, lnk, cx, v)
def setup_inputs_ties(rng):
    cnt, ptr, suf, lnk, cx, v = parts(rng)
    rows = np.array([4, 1, 2, 8, 1, 0, 16, 4, 8, 8, 16]); vals = np.array([3, 1, 1, 1, 15, 0, 15, 1, 3, 7, 3]); k = rng.integers(0, 11, (N, 8, W0))
    order = np.argsort(rng.random((N, 8, W0, 16)), axis=-1)
    cnt = np.where(order < rows[k][..., None], vals[k][..., None], 0).transpose(0, 1, 3, 2)
    v = np.where(rng.random(v.shape) < 0.6, 16 * rng.integers(0, 17, v.shape), 15 * rng.integers(0, 18, v.shape)) + np.where(rng.random(v.shape) < 0.6, 0, rng.integers(-1, 2, v.shape))
    return pack(cnt, ptr, suf, lnk, cx, np.minimum(np.maximum(v, 0), 255))
def setup_inputs_alike(rng):
    cnt, ptr, suf, lnk, cx, v = parts(rng); few = rng.integers(1, W0, (N, 8, 6))
    def some(n, m):
        return np.take_along_axis(few, rng.integers(0, m, (N, 8, n)), 2)
    ptr = some(16 * W0, 6).reshape(N, 8, 16, W0); suf = np.where(rng.random((N, 8, W0)) < 0.5, some(W0, 6), suf); lnk = np.where(rng.random((N, 8, W0)) < 0.5, some(W0, 6), lnk); cx = some(LN, 4)
    levels(rng, cnt, suf, v, 3); cx[:, 3, :B] = rng.choice(np.array([70, W0 - 1]), (N, B))
    cx[:, 5] = cx[:, 5, :1]; v[:, 5] = v[:, 5, :, :1]
    filled(rng, cnt, ptr, suf, lnk, cx, v, 2); kept(rng, cnt, ptr, suf, cx, v, 6); clones(rng, cnt, ptr, suf, lnk, cx, v, 7)
    return pack(cnt, ptr, suf, lnk, cx, v)
def setup_inputs_ends(rng):
    cnt, ptr, suf, lnk, cx, v = parts(rng); e = np.array([0, 1, W0 - 1])
    ptr = np.where(rng.random(ptr.shape) < 0.3, rng.choice(e, ptr.shape), ptr); lnk = np.where(rng.random(lnk.shape) < 0.5, rng.choice(e, lnk.shape), lnk); cx = np.where(rng.random(cx.shape) < 0.5, rng.choice(e, cx.shape), cx)
    suf[:, 1::2] = np.where(rng.random((N, 4, W0)) < 0.3, np.arange(W0), rng.integers(0, W0, (N, 4, W0))); suf[:, 2] = 0; suf[:, 4] = 0; suf[:, 5] = 0
    cnt[:, 4, :, 0] = 0; cnt[:, 5, :, 0] = 15; cnt[:, 6] = 15 * (cnt[:, 6] > 0); cnt[:, 7, :, W0 - 1] = 0; cnt[:, 0, :, W0 - 1] = 15
    v = np.where(rng.random(v.shape) < 0.7, rng.choice(np.array([0, 1, 127, 128, 239, 240, 254, 255]), v.shape), v)
    return pack(cnt, ptr, suf, lnk, cx, v)
def setup_inputs_spread(rng):
    def low(*shape):
        return np.minimum((W0 * rng.random(shape) ** rng.integers(1, 5, shape[:2] + (1,) * (len(shape) - 2))).astype(np.int64), W0 - 1)
    cnt = np.where(rng.random((N, 8, 16, W0)) < rng.random((N, 8, 1, W0)) ** 2, np.minimum(np.exp2(4 * rng.random((N, 8, 16, W0)) * rng.random((N, 8, 1, W0)) ** 0.5).astype(np.int64), 15), 0)
    v = np.minimum((256 * rng.random((N, 8, RO * SP, LN)) ** 3).astype(np.int64), 255)
    return pack(cnt, low(N, 8, 16, W0), low(N, 8, W0), W0 - 1 - low(N, 8, W0), low(N, 8, LN), np.where(rng.random(v.shape) < 0.5, v, 255 - v))
def check_inputs(d):
    bad = []
    for k, hi in (("tab", 16 * W0 - 1), ("suf", W0 - 1), ("lnk", W0 - 1), ("cx", W0 - 1)):
        if np.min(d[k]) < 0 or np.max(d[k]) > hi: bad.append("range of " + k)
    v = np.asarray(d["vv"]).astype(np.float32)
    if not np.all((v >= 0) & (v <= 255) & (v == np.floor(v))): bad.append("range of vv")
    return bad
def reference(tab, suf, lnk, cx, vv):
    k = tab.astype(np.int32).reshape(N, 8, 16, W0)
    C = np.zeros((N, 8, 16, W), np.int32); S = np.zeros((N, 8, 16, W), np.int32); C[..., :W0] = k & 15; S[..., :W0] = k >> 4
    F = np.zeros((N, 8, W), np.int32); L = np.zeros((N, 8, W), np.int32); F[..., :W0] = suf; L[..., :W0] = lnk
    v = vv.astype(np.float32).astype(np.int32).reshape(N, 8, RO, SP, 1, LN)
    c = np.stack([gentries(a) for a in cx]).astype(np.int32); e = np.zeros((N, 8, 16, LN), np.int32); f = np.full((N, 8, LN), -1, np.int32)
    qi = np.arange(N)[:, None, None]; gi = np.arange(8)[None, :, None]
    for t in range(RO):
        for s in range(SP):
            cc = np.take_along_axis(C, c[:, :, None, :], 3)
            n = cc * (1 - e); P = np.add.accumulate(n, axis=2, dtype=np.int32); E = np.add.reduce((n > 0).astype(np.int32), axis=2)
            z = np.add.reduce((256 * P <= v[:, :, t, s] * (P[:, :, 15] + E)[:, :, None, :]).astype(np.int32), axis=2)
            z = np.where(c == 0, np.minimum(z, 15), z); esc = z == 16
            d, fb = c, f
            f = np.where(esc, np.where(fb < 0, d, fb), -1)
            e = np.where(esc[:, :, None, :], np.maximum(e, (cc > 0).astype(np.int32)), 0)
            c = np.where(esc, F[qi, gi, d], S[qi, gi, np.minimum(z, 15), d])
        for q in range(N):
            for g in range(8):
                j = np.nonzero(~esc[q, g, :B] & (fb[q, g, :B] >= 0))[0]
                a = j[np.unique(fb[q, g, j], return_index=True)[1]]
                w = W0 + B * t + a; to = c[q, g, a]
                cw = (C[q, g][:, to] + 1) >> 1; sw = S[q, g][:, to]
                C[q, g][:, w] = cw; S[q, g][:, w] = sw; F[q, g, w] = to; L[q, g, w] = L[q, g, to]
                C[q, g, z[q, g, a], fb[q, g, a]] = 1; S[q, g, z[q, g, a], fb[q, g, a]] = w
                b = j[np.unique(d[q, g, j], return_index=True)[1]]
                C[q, g, z[q, g, b], d[q, g, b]] = np.minimum(15, C[q, g, z[q, g, b], d[q, g, b]] + 1)
        slot = esc & (np.add.accumulate(esc.astype(np.int32), axis=2) <= CAP)
        c2 = np.array(c); e2 = np.array(e); f2 = np.array(f)
        for r in range(N):
            q = (r - 1) % N
            for g in range(8):
                a = np.nonzero(slot[q, g])[0]; b = np.nonzero(slot[r, g])[0]; m = min(len(a), len(b)); a = a[:m]; b = b[:m]
                c2[r, g, b] = L[q, g, c[q, g, a]]; e2[r, g][:, b] = e[q, g][:, a]; f2[r, g, b] = -1
        c, e, f = c2, e2, f2
    return {"yn": C.reshape(N, 128, W).astype(np.float32).astype(BF), "yc": np.stack([gtable(a) for a in c]).astype(np.float32)}

@@ -1,0 +1,552 @@
+from concourse.mybir import AluOpType as O, ActivationFunctionType as AF
+
+W0, B, LN, RO, SP, CAP = 3328, 256, 2048, 3, 3, 512
+TW = 4352
+D = 2.0 ** -14
+MAG = 1.5 * 2.0 ** 27
+NCH, CH = 4, 832
+
+
+def _sb(dtype, **shapes):
+    return {k: ("sbuf", [128] + ([n] if n > 0 else [16, -n]), dtype) for k, n in shapes.items()}
+
+
+SCRATCH = {}
+SCRATCH.update(_sb("int32", tk=W0, ti0=CH, ti1=CH, ip=128, im=128, pg=128, mg=128, pm=128, mm=128, io3=-16, sfi=208, lki=208, lkj=208, cxi=128, rr=256))
+SCRATCH.update(_sb("float32", TC=TW, TS=2 * TW, TL=4096, vl=384, Sg=LN, MK=640, sm=176, RS=16, RSn=16, dif=128, mrow=512, krow=128,
+                   mi=32, mL=32, Dm=32, wr0=256, wr1=256, wr2=256, zz=128, cols=16, sff=208, lhf=208, llf=208, cf=128, nz=128, c2f=128,
+                   xx=128, es=128, x2=128, o1=32, o2=32, uf=256, nu=256, u1=256, uw=256, r2=256, aC=256, aS=256,
+                   inc=128, X=128, ha=128, hb=128, hc=128, Yl=128, lnf=32, tot=8, lT0=8, lT1=8, lT2=8, vd=32, so=32, mvv=128, nmv=128))
+SCRATCH.update(_sb("bfloat16", vvr=SP * LN, G=LN, cm=LN, mk=LN + CAP, H=LN + CAP, EQ=-256, yb=4096, ES=-128, Dn=-128, D15=-128, EV=-128, EW=-128,
+                   EH=-128, BO=128, PRE=128, ZT=128, DL=128, BN=128, B15=128, cc=640, tri=-16, eb=128, cr=512, fr=512, OH=512, MS=512, Lg=512,
+                   lM0=512, lM1=512, lL0=512, lL1=512, lL2=512))
+SCRATCH.update(_sb("float16", q=LN, Y=LN, th=128, mmB=128, mm1=128, mmV=128, mv1=128, kh=64, R=512, off=128, kr=512, CG=512))
+SCRATCH.update(_sb("uint16", cu=128, cu2=128, ou=32, ofu=8, klu=32, cmu=32, lnu=32, sou=32))
+SCRATCH.update({k: ("psum", [128, n], "float32") for k, n in (("PX0", 1024), ("PX1", 1024), ("PU", 1024), ("PL0", 512), ("PL1", 512))})
+DMAS = ["d%d" % i for i in range(24)]
+REM = [a + str(t) for t in range(RO) for a in ("aT", "aM", "aL", "nT", "nM", "nL") if not (t == RO - 1 and a[1] == "M")]
+SEMAPHORES = ["sV", "sA", "sP", "sG"] + DMAS + REM
+BANKS = {"PX00", "PX01", "PX10", "PX11", "PU0", "PU1", "PL0", "PL1"}
+
+
+def rank_program(g, core, T, topo):
+    rank = T.rank_of(core)
+    if rank is None:
+        return
+    V, A, P, S = g.vector, g.scalar, g.tensor, g.sync
+    eng = {"V": V, "A": A, "P": P, "S": S, "G": g}
+    seen = {k: {} for k in eng}
+    cnt = {k: 0 for k in "VAPG"}
+    wr, rd, left = {}, {}, {}
+    ndma = [0]
+
+    def run(qn, fn, r, w, acc=False, sem=None, remote=False, n=1):
+        r, w = r.split(), w.split()
+        own = "s" + qn
+        need = {}
+
+        def want(toks, skip):
+            for s, v in toks.items():
+                if not (skip and s == own):
+                    need[s] = max(need.get(s, 0), v)
+        for k in r:
+            want(wr.get(k, {}), False)
+            if k in BANKS:
+                want(rd.get(k, {}), True)
+        for k in w:
+            want(wr.get(k, {}), acc)
+            want(rd.get(k, {}), sem is None)
+        for s in sorted(need):
+            if seen[qn].get(s, 0) < need[s]:
+                eng[qn].wait_ge(T.sem[s], need[s])
+                seen[qn][s] = need[s]
+        inst = fn()
+        if sem is None:
+            cnt[qn] += 1
+            s, v = own, cnt[qn]
+        else:
+            s, v = sem, n
+        if not remote:
+            inst.then_inc(T.sem[s], n)
+        left[s] = v
+        for k in r:
+            rd.setdefault(k, {})[s] = v
+        for k in w:
+            wr[k] = {s: v}
+            rd[k] = {}
+
+    def v_(fn, r, w): run("V", fn, r, w)
+    def a_(fn, r, w): run("A", fn, r, w)
+    def p_(fn, r, w): run("P", fn, r, w, acc=True)
+    def g_(fn, r, w): run("G", fn, r, w)
+
+    def dma(qn, out, in_, r, w):
+        s = DMAS[ndma[0]]
+        ndma[0] += 1
+        run(qn, lambda: eng[qn].dma_start(out, in_), r, w, sem=s, n=16)
+
+    def ts(out, in0, s1, op0, r, w, s2=None, op1=None):
+        if op1 is None:
+            v_(lambda: V.tensor_scalar(out, in0, s1, None, op0), r, w)
+        else:
+            v_(lambda: V.tensor_scalar(out, in0, s1, s2, op0, op1), r, w)
+
+    def tt(out, in0, in1, op, r, w):
+        v_(lambda: V.tensor_tensor(out, in0, in1, op), r, w)
+
+    def cp(out, in_, r, w):
+        v_(lambda: V.tensor_copy(out, in_), r, w)
+
+    def act(out, in_, func, r, w, bias=0.0, scale=1.0):
+        a_(lambda: A.activation(out, in_, func, bias=bias, scale=scale), r, w)
+
+    def listsum(out, fam, src, lo, hi, r, w, start=True, stop=True):
+        def f():
+            for i in range(16):
+                x = P.matmul(out, fam[:, i, :], src[:, lo + i:hi:16], start and i == 0, stop and i == 15)
+            return x
+        p_(f, r, w)
+
+    def spread(out, base, n, fam, src, lo, r, w, start=True):
+        def f():
+            for i in range(16):
+                x = P.matmul(out[:, base + i:base + n:16], fam[:, i, :], src[:, lo:lo + n // 16], start, start or i == 15)
+            return x
+        p_(f, r, w)
+
+    nxt = T.cores[(rank + 1) % len(T.cores)]
+    rid, pid, _se = topo.addr(nxt)
+    emask = topo.mask(core, nxt)
+    ne = len(topo.engines(core, nxt))
+
+    def send(dst, src, name, t, r):
+        s, rs = "n%s%d" % (name, t), "a%s%d" % (name, t)
+        run("G", lambda: g.remote_dma(dst, src, T.sem[rs], T.sem[s], pid, rid, emask), r, "", sem=s, remote=True, n=ne)
+
+    for t in range(RO):
+        for a in "TML":
+            if t < RO - 1 or a != "M":
+                wr["l%s%d" % (a, t)] = {"a%s%d" % (a, t): ne}
+                left["a%s%d" % (a, t)] = ne
+
+    def sm(k):
+        return T.sm[:, 16 * k:16 * k + 16]
+
+    def cc(k):
+        return T.cc[:, 128 * k:128 * k + 128]
+
+    def loadv(qn, t):
+        dma(qn, T.vvr[0:8, :], T.vv[:, SP * LN * t:SP * LN * (t + 1)], "", "vvr")
+
+    def vlist(t):
+        for s in range(SP):
+            def f(s=s):
+                for i in range(16):
+                    x = P.matmul(T.PU[:, 512 + 128 * s:640 + 128 * s], T.EV[0:8, i, :], T.vvr[0:8, LN * s + i:LN * (s + 1):16], i == 0, i == 15)
+                return x
+            p_(f, "EV vvr", "PU1")
+        act(T.vl[:], T.PU[:, 512:512 + 128 * SP], AF.Copy, "PU1", "vl", scale=1.0 / 256)
+
+    loadv("A", 0)
+    for k in range(NCH):
+        dma("S", T.tk[:, k * CH:(k + 1) * CH], T.tab[:, k * CH:(k + 1) * CH], "", "tk%d" % k)
+        if k == 0:
+            dma("S", T.cxi[:], T.cx[:, :], "", "cxi")
+            dma("S", T.sfi[:], T.suf[:, :], "", "sfi")
+    dma("S", T.lki[:], T.lnk[:, :], "", "lki")
+
+    def iota(out, pat, base, cm, w, small=True):
+        if small:
+            g_(lambda: g.iota(out, pat, base, cm, allow_small_or_imprecise_dtypes=True), "", w)
+        else:
+            g_(lambda: g.iota(out, pat, base, cm), "", w)
+    iota(T.ip[:], [[0, 128]], 0, 1, "ip", False)
+    iota(T.im[:], [[1, 128]], 0, 0, "im", False)
+    iota(T.TS[:, TW:TW + 2176], [[0, 2176]], 0, 0, "TSF0")
+    iota(T.TS[:, TW + 2176:2 * TW], [[0, 2176]], 0, 0, "TSF1")
+    iota(T.TC[:, W0:TW], [[0, TW - W0]], 0, 0, "TCz")
+    iota(T.TS[:, W0:TW], [[0, TW - W0]], 0, 0, "TSz")
+    iota(T.mi[:], [[16, 32]], 129, 0, "mi")
+    iota(T.io3[:], [[0, 16], [1, 16]], 0, 0, "io3", False)
+    iota(T.krow[:], [[1, 128]], 0, 0, "krow")
+    iota(T.TL[:], [[0, 4096]], 0, 0, "TL")
+    iota(T.mrow[:], [[1, 512]], 129, 0, "mrow")
+    for t in range(RO):
+        iota(T["wr%d" % t][:], [[1, 256]], W0 + B * t - 2048, 0, "wr%d" % t)
+    iota(T.H[:, LN:], [[0, CAP]], 0, 0, "H")
+
+    ts(T.pg[:], T.ip[:], 4, O.arith_shift_right, "ip", "pg")
+    ts(T.mg[:], T.im[:], 4, O.arith_shift_right, "im", "mg")
+    ts(T.pm[:], T.ip[:], 15, O.bitwise_and, "ip", "pm")
+    ts(T.mm[:], T.im[:], 15, O.bitwise_and, "im", "mm")
+    tt(T.BO[:], T.pg[:], T.mg[:], O.is_equal, "pg mg", "BO")
+    tt(T.RS[:], T.pm[:, 0:16], T.mm[:, 0:16], O.is_equal, "pm mm", "RS")
+    ts(T.mm1[:], T.mm[:], 1.0, O.add, "mm", "mm1")
+    tt(T.mv1[:], T.mg[:], T.ip[:], O.is_equal, "mg ip", "mv1")
+    ts(T.RSn[:], T.RS[:], -1.0, O.mult, "RS", "RSn")
+    tt(T.mv1[:], T.mv1[:], T.mm1[:], O.mult, "mv1 mm1", "mv1")
+    tt(T.mm1[:], T.mm1[:], T.BO[:], O.mult, "mm1 BO", "mm1")
+    ts(T.mmV[:], T.mv1[:], -1.0, O.add, "mv1", "mmV")
+    ts(T.mmB[:], T.mm1[:], -1.0, O.add, "mm1", "mmB")
+    for i in range(16):
+        ts(T.EV[0:8, i, :], T.mmV[0:8, :], float(i), O.is_equal, "mmV", "EV%d" % i)
+    for i in range(16):
+        ts(T.ES[:, i, :], T.mmB[:], float(i), O.is_equal, "mmB", "ES%d" % i)
+    wr["EV"] = wr["EV15"]
+    wr["ES"] = wr["ES15"]
+    for i in range(16):
+        act(T.Dn[:, i, :], T.BO[:], AF.Copy, "BO RSn", "Dn%d" % i, scale=T.RSn[:, i:i + 1])
+    wr["Dn"] = wr["Dn15"]
+    cu, cf, nz = T.cu, T.cf, T.nz
+    cp(cu[:], T.cxi[:], "cxi", "cu0 cu1")
+    cp(cf[:], T.cxi[:], "cxi", "cf0 cf1")
+    ts(T.sff[:], T.sfi[:], -2048.0, O.add, "sfi", "sff")
+    ts(nz[:], cf[:], 0.5, O.is_gt, "cf0 cf1", "nz0 nz1", float(TW), O.mult)
+    dma("S", T.TS[15:128:16, TW:TW + W0], T.sff[:], "sff TSF0 TSF1", "TSF")
+    vlist(0)
+    tt(cc(4), T.ip[:], T.im[:], O.is_le, "ip im", "c4")
+    tt(T.dif[:], T.im[:], T.ip[:], O.subtract, "im ip", "dif")
+    tt(T.PRE[:], T.BO[:], cc(4), O.mult, "BO c4", "PRE")
+    ts(cc(0), T.dif[:], 1.0, O.is_equal, "dif", "c0")
+    ts(cc(1), T.dif[:], -15.0, O.is_equal, "dif", "c1")
+    tt(T.ZT[:], T.PRE[:], T.BO[:], O.subtract, "PRE BO", "ZT")
+    ts(cc(2), T.dif[:], 0.0, O.is_equal, "dif", "c2")
+    tt(cc(0), cc(0), cc(1), O.add, "c0 c1", "c0")
+    ts(cc(3), T.mm[:], 15.0, O.is_lt, "mm", "c3")
+    tt(cc(0), cc(0), T.BO[:], O.mult, "c0 BO", "c0")
+    tt(cc(2), cc(2), cc(3), O.mult, "c2 c3", "c2")
+    ts(T.BN[:], T.BO[:], T.RS[:, 15:16], O.mult, "BO RS", "BN", 1024.0, O.mult)
+    tt(T.DL[:], cc(0), cc(2), O.subtract, "c0 c2", "DL")
+    ts(T.cols[:, 0:1], T.RS[:, 15:16], 800.0, O.mult, "RS", "cl0", -400.0, O.add)
+    ts(T.cols[:, 1:2], T.RS[:, 15:16], 1609800.0, O.mult, "RS", "cl1", -409800.0, O.add)
+    ts(T.cols[:, 2:3], T.pm[:, 0:1], 0.0, O.add, "pm", "cl2")
+    ts(T.cols[:, 3:4], T.RS[:, 0:1], 64.0, O.mult, "RS", "cl3a")
+    tt(T.cols[:, 4:5], T.cols[:, 3:4], T.RS[:, 1:2], O.add, "cl3a RS", "cl3")
+    for k in range(NCH):
+        sl = slice(k * CH, (k + 1) * CH)
+        ti, tn = T["ti%d" % (k % 2)], "ti%d" % (k % 2)
+        ts(ti[:], T.tk[:, sl], 15, O.bitwise_and, "tk%d" % k, tn)
+        ts(T.TC[:, sl], ti[:], -D, O.add, tn, "TC_%d" % k)
+
+    def tables2():
+        for k in range(NCH):
+            sl = slice(k * CH, (k + 1) * CH)
+            ts(T.TS[:, sl], T.tk[:, sl], -7.5, O.add, "tk%d" % k, "TS_%d" % k, MAG, O.add)
+            act(T.TS[:, sl], T.TS[:, sl], AF.Identity, "TS_%d" % k, "TS_%d" % k, bias=-(MAG / 16) - 2048.0, scale=1.0 / 16)
+    tables2()
+    v_(lambda: V.memset(sm(0), 0.0), "", "F1")
+
+    def late():
+        v_(lambda: V.memset(T.zz[:], 0.0), "", "zz")
+        ts(T.lkj[:], T.lki[:], 6, O.arith_shift_right, "lki", "lkj")
+        ts(T.lki[:], T.lki[:], 63, O.bitwise_and, "lki", "lki")
+        cp(T.lhf[:], T.lkj[:], "lkj", "lhf")
+        cp(T.llf[:], T.lki[:], "lki", "llf")
+        dma("S", T.TL[0:128:16, 0:W0], T.lhf[:], "lhf TL", "TLa")
+        dma("S", T.TL[1:128:16, 0:W0], T.llf[:], "llf TL", "TLb")
+        ts(cc(3), T.mm[:], 15.0, O.is_equal, "mm", "c3")
+        ts(T.tri[:], T.io3[:], T.cols[:, 2:3], O.is_gt, "io3 cl2", "tri")
+        tt(T.B15[:], T.BO[:], cc(3), O.mult, "BO c3", "B15")
+        ts(T.mL[:], T.mi[:], T.cols[:, 2:3], O.add, "mi cl2", "mL")
+        for i in range(16):
+            ts(T.EW[:, i, :], T.mmB[:], float(i), O.is_equal, "mmB cl2", "EW%d" % i, T.cols[:, 2:3], O.mult)
+            ts(T.EH[:, i, :], T.mmB[:], float(i), O.is_equal, "mmB cl3", "EH%d" % i, T.cols[:, 4:5], O.mult)
+        wr["EW"] = wr["EW15"]
+        wr["EH"] = wr["EH15"]
+        ts(T.Dm[:], T.mL[:], float(LN - 129), O.add, "mL", "Dm")
+        ts(sm(9), T.mL[:, 0:16], float(4096 - 129 - 2047), O.add, "mL", "bz")
+        ts(sm(10), sm(9), 2047.0, O.add, "bz", "bz16", 16.0, O.mult)
+
+    def late_a():
+        for i in range(16):
+            act(T.D15[:, i, :], T.B15[:], AF.Copy, "B15 RSn", "D15%d" % i, scale=T.RSn[:, i:i + 1])
+        wr["D15"] = wr["D1515"]
+
+    TCR = "TC TC_0 TC_1 TC_2 TC_3 TCz"
+    TSR = "TS TS_0 TS_1 TS_2 TS_3 TSz TSF TSF0 TSF1"
+    TLR = "TL TLa TLb"
+    Wt = [W0]
+    PX, PL = (T.PX0, T.PX1), (T.PL0, T.PL1)
+
+    def K(s, h):
+        return s.replace("@", str(h))
+
+    def HL(h):
+        return slice(1024 * h, 1024 * h + 1024)
+
+    def HC(h):
+        return slice(64 * h, 64 * h + 64)
+
+    def S1(h, t, s):
+        win = T.TC[:, 0:Wt[0]].indirect(cu[:, HC(h)])
+        if t == 0 and s == 0:
+            cp(T.q[:, HL(h)], win, TCR + K(" cu@", h), K("q@", h))
+        else:
+            tt(T.q[:, HL(h)], win, T.mk[:, HL(h)], O.mult, TCR + K(" cu@ mk@", h), K("q@", h))
+
+    def S3q(h):
+        listsum(PL[h][:, 0:64], T.ES, T.q, 1024 * h, 1024 * h + 1024, K("q@ ES", h), K("PL@", h))
+
+        def f():
+            for b in (0, 512):
+                x = P.matmul(PX[h][:, b:b + 512], T.PRE[:], T.q[:, 1024 * h + b:1024 * h + b + 512], True, False)
+            return x
+        p_(f, K("q@ PRE", h), K("PX@0 PX@1", h))
+        listsum(PL[h][:, 64:128], T.ES, T.q, 1024 * h, 1024 * h + 1024, K("q@ ES", h), K("PL@", h), stop=False)
+
+    def S2(h):
+        act(T.G[:, HL(h)], T.q[:, HL(h)], AF.Sigmoid, K("q@", h), K("G@", h), bias=-200.0, scale=400.0)
+
+    def S3G(h):
+        listsum(PL[h][:, 64:128], T.ES, T.G, 1024 * h, 1024 * h + 1024, K("G@ ES", h), K("PL@", h), start=False)
+
+    def S4(h, s):
+        C = HC(h)
+        tt(T.xx[:, C], PL[h][:, 64:128], T.vl[:, 128 * s + 64 * h:128 * s + 64 * h + 64], O.mult, K("PL@ vl", h), K("xx@", h))
+        tt(T.es[:, C], PL[h][:, 0:64], T.xx[:, C], O.is_le, K("PL@ xx@", h), K("es@", h))
+        tt(T.es[:, C], T.es[:, C], nz[:, C], O.mult, K("es@ nz@", h), K("es@", h))
+        tt(T.c2f[:, C], cf[:, C], T.es[:, C], O.add, K("cf@ es@", h), K("c2f@", h))
+        tt(T.x2[:, C], T.xx[:, C], T.es[:, C], O.add, K("xx@ es@", h), K("x2@", h))
+        cp(T.cu2[:, C], T.c2f[:, C], K("c2f@", h), K("cu2@", h))
+        ts(T.th[:, C], T.x2[:, C], 1025.0 - 0.4975, O.add, K("x2@", h), K("th@", h))
+
+    def flist(s):
+        ts(sm(5), T.es[:, 0:16], 0.5, O.is_gt, "es0", "e01")
+        ts(sm(1), cf[:, 0:16], 1.0, O.add, "cf0", "d1")
+        ts(sm(2), sm(0), 0.5, O.is_lt, "F1", "t1")
+        tt(sm(3), sm(2), sm(1), O.mult, "t1 d1", "t2")
+        tt(sm(4), sm(0), sm(3), O.add, "F1 t2", "Fo")
+        if s == SP - 1:
+            tt(sm(2), sm(0), sm(5), O.mult, "F1 e01", "t1")
+            tt(sm(3), sm(0), sm(2), O.subtract, "F1 t1", "t2")
+            ts(sm(6), sm(3), 0.5, O.is_gt, "t2", "ca")
+            ts(sm(7), sm(3), -2048.0, O.add, "t2", "kf")
+            tt(sm(2), sm(1), sm(6), O.mult, "d1 ca", "t1")
+            ts(T.kh[:, 0:16], sm(7), -1.0, O.mult, "kf", "kh0")
+            ts(sm(8), sm(2), -2048.0, O.add, "t1", "kd")
+            ts(T.kh[:, 16:32], sm(8), -1.0, O.mult, "kd", "kh1")
+        tt(sm(0), sm(4), sm(5), O.mult, "Fo e01", "F1")
+
+    def S5(h):
+        act(T.Sg[:, HL(h)], T.TS[:, 0:TW + Wt[0]].indirect(T.cu2[:, HC(h)]), AF.Copy, TSR + K(" cu2@", h), K("Sg@", h))
+
+    def P6(h):
+        for b in (0, 1):
+            spread(PX[h], 512 * b, 512, T.Dn, T.th, 64 * h + 32 * b, K("th@ Dn", h), K("PX@%d" % b, h), start=False)
+
+    def S7(h):
+        act(T.cm[:, HL(h)], PX[h][:], AF.Sigmoid, K("PX@0 PX@1 cl0 cl1", h), K("cm@", h), bias=T.cols[:, 1:2], scale=T.cols[:, 0:1])
+
+    def P8(h, marks):
+        def f(ps, lhs):
+            for b in (0, 512):
+                x = P.matmul(ps[:, b:b + 512], lhs[:], T.cm[:, 1024 * h + b:1024 * h + b + 512], True, True)
+            return x
+        p_(lambda: f(T.PU, T.DL), K("cm@ DL", h), "PU0 PU1")
+        if marks:
+            p_(lambda: f(PX[h], T.BN), K("cm@ BN", h), K("PX@0 PX@1", h))
+
+    def S9(h, s):
+        tt(T.Y[:, HL(h)], T.Sg[:, HL(h)], T.PU[:], O.mult, K("Sg@ PU0 PU1", h), K("Y@", h))
+        if s == SP - 1 and h == 0:
+            act(T.uf[:], T.PU[:, 0:256], AF.Copy, "PU0", "uf")
+
+    def S10(h):
+        listsum(PL[h][:, 128:192], T.ES, T.Y, 1024 * h, 1024 * h + 1024, K("Y@ ES", h), K("PL@", h))
+
+    def M(h):
+        tt(T.mk[:, HL(h)], T.q[:, HL(h)], PX[h][:], O.is_lt, K("q@ PX@0 PX@1", h), K("mk@", h))
+
+    def S11(h):
+        C, y = HC(h), PL[h][:, 128:192]
+        ts(cu[:, C], y, 2048.0, O.add, K("PL@", h), K("cu@", h))
+        ts(cf[:, C], y, 2048.0, O.add, K("PL@", h), K("cf@", h))
+        ts(nz[:, C], y, -2047.5, O.is_gt, K("PL@", h), K("nz@", h), float(TW), O.mult)
+
+    for t in range(RO):
+        last = t == RO - 1
+        iota(T.MK[:], [[0, 640]], 0, 0, "MK")
+        iota(T.H[:, 0:LN], [[0, LN]], 0, 0, "H")
+        for s in range(SP):
+            marks = not (last and s == SP - 1)
+            S1(0, t, s)
+            S3q(0)
+            if s:
+                S9(1, s - 1)
+                S10(1)
+                M(1)
+            S2(0)
+            S3G(0)
+            if s:
+                S11(1)
+            S4(0, s)
+            S5(0)
+            P6(0)
+            S7(0)
+            P8(0, marks)
+            S1(1, t, s)
+            S3q(1)
+            flist(s)
+            if t == 0 and s == 0:
+                late()
+            S9(0, s)
+            S10(0)
+            if marks:
+                M(0)
+            S2(1)
+            S3G(1)
+            S11(0)
+            S4(1, s)
+            S5(1)
+            P6(1)
+            S7(1)
+            if s < SP - 1:
+                P8(1, marks)
+            if t == 0 and s == 0:
+                late_a()
+        if not last:
+            loadv("S", t + 1)
+        tot = T.PX0[:, 0:128]
+        ts(T.eb[:], T.es[:], 0.5, O.is_gt, "es0 es1", "eb")
+        p_(lambda: P.matmul(tot, T.BO[:], T.eb[:], True, True), "BO eb", "PX00")
+        p_(lambda: P.matmul(T.PX0[:, 512:640], T.ZT[:], T.eb[:], True, True), "ZT eb", "PX01")
+        spread(T.PL0, 256, 256, T.Dn, T.kh, 0, "Dn kh0", "PL0")
+        spread(T.PL1, 256, 256, T.Dn, T.kh, 16, "Dn kh1", "PL1")
+        v_(lambda: V.tensor_tensor_scan(T.inc[:], tot, T.zz[:], 128.0, O.add, O.add), "PX00 zz", "inc")
+        ts(T.hc[:], tot, 0.5, O.is_gt, "PX00", "hc")
+        tt(T.ha[:], T.inc[:], tot, O.subtract, "inc PX00", "ha")
+        tt(T.X[:], T.inc[:], T.PX0[:, 512:640], O.add, "inc PX01", "X")
+        ts(T.hb[:], T.ha[:], 639.5, O.is_lt, "ha", "hb")
+        tt(T.ha[:], T.ha[:], T.hc[:], O.mult, "ha hc", "ha")
+        tt(T.ha[:], T.ha[:], T.hb[:], O.mult, "ha hb", "ha")
+        tt(T.off[:], T.ha[:], T.krow[:], O.max, "ha krow", "off")
+        listsum(T.PX0[:, 0:8], T.ES, T.off, 0, 128, "off ES", "PX00")
+        P8(1, marks)
+        ts(T.tot[:, 0:1], T.inc[:, 127:128], -128.0, O.add, "inc", "tot")
+        send(T["lT%d" % t][:, 0:1], T.tot[:, 0:1], "T", t, "tot")
+        tt(T.X[:], T.X[:], T.eb[:], O.mult, "X eb", "X")
+        cp(T.R[:, 0:256], T.PL0[:, 256:512], "PL0", "R0")
+        ts(T.ofu[:], T.PX0[:, 0:8], 1.0 / 16, O.mult, "PX00", "ofu")
+        cp(T.MK[:, 0:640].indirect(T.ofu[:]), T.krow[:], "krow ofu", "MK")
+        cp(T.R[:, 256:512], T.PL1[:, 256:512], "PL1", "R1")
+        v_(lambda: V.tensor_tensor_scan(T.kr[:], T.MK[:, 128:640], T.MK[:, 128:640], 0.0, O.max, O.max), "MK", "kr")
+        S9(1, SP - 1)
+        S10(1)
+        listsum(T.PX0[:, 0:32], T.ES, T.kr, 0, 512, "kr ES", "PX00")
+        if marks:
+            M(1)
+        ts(T.nu[:], T.uf[:], -1.0, O.mult, "uf", "nu", 1.0, O.add)
+        S11(1)
+        ts(T.klu[:], T.PX0[:, 0:32], 1.0 / 16, O.mult, "PX00", "klu")
+        ts(T.Yl[:], cf[:], -2048.0, O.add, "cf0 cf1", "Yl")
+        tt(T.OH[:], T.X[:].indirect(T.klu[:]), T.mrow[:], O.is_equal, "X klu mrow", "OH")
+        tt(T.CG[:], T.Yl[:].indirect(T.klu[:]), T.OH[:], O.mult, "Yl klu OH", "CG")
+        if marks:
+            listsum(T.PX0[:, 0:32], T.ES, T.kr, 0, 512, "kr ES", "PX00", stop=False)
+            listsum(T.PX0[:, 0:32], T.EW, T.OH, 0, 512, "OH EW", "PX00", start=False)
+            listsum(T.PX0[:, 512:544], T.ES, T.CG, 0, 512, "CG ES", "PX01")
+        else:
+            listsum(T.PX0[:, 512:544], T.ES, T.CG, 0, 512, "CG ES", "PX01")
+            listsum(T.PX0[:, 0:32], T.ES, T.kr, 0, 512, "kr ES", "PX00", stop=False)
+            listsum(T.PX0[:, 0:32], T.EW, T.OH, 0, 512, "OH EW", "PX00", start=False)
+        ts(T.u1[:], T.uf[:], 1.0 - D, O.mult, "uf", "u1")
+
+        def dups(x):
+            kk, R, kn = 112 + 16 * x, T.R, ("kf", "kd")[x]
+            for k in range(16):
+                ts(T.EQ[:, k, 0:256 - 16 * k], R[:, 256 * x + 16 * k:256 * x + 256], T.sm[:, kk + k:kk + k + 1], O.is_equal, "R%d %s" % (x, kn), "EQ%d" % k)
+            alle = " ".join("EQ%d" % k for k in range(16))
+            tt(T.EQ[:, :, 0:16], T.EQ[:, :, 0:16], T.tri[:], O.mult, alle + " tri", alle)
+
+            def f():
+                for k in range(16):
+                    y = P.matmul(PL[x][:, 256 + 16 * k:512], T.BO[:], T.EQ[:, k, 0:256 - 16 * k], k == 0, k == 15)
+                return y
+            p_(f, alle + " BO", "PL%d" % x)
+            ts(T.cr[:, 256 * x:256 * x + 256], R[:, 256 * x:256 * x + 256], -2047.5, O.is_gt, "R%d" % x, "cr%d" % x)
+
+        def firsts(x):
+            sl = slice(256 * x, 256 * x + 256)
+            tt(T.fr[:, sl], PL[x][:, 256:512], T.cr[:, sl], O.is_lt, "PL%d cr%d" % (x, x), "fr%d" % x)
+            listsum(PL[x][:, 192:208], T.ES, T.fr, 256 * x, 256 * x + 256, "fr%d ES" % x, "PL%d" % x)
+
+        def offs(x):
+            kk, o, kn = 7 + x, slice(16 * x, 16 * x + 16), ("kf", "kd")[x]
+            tt(T.o1[:, o], sm(kk), sm(9), O.subtract, kn + " bz", "o1%d" % x)
+            tt(T.o2[:, o], T.o1[:, o], PL[x][:, 192:208], O.mult, "o1%d PL%d" % (x, x), "o2%d" % x)
+            tt(T.o1[:, o], T.o2[:, o], sm(10), O.add, "o2%d bz16" % x, "o1%d" % x)
+            ts(T.ou[:, o], T.o1[:, o], 1.0 / 16, O.mult, "o1%d" % x, "ou%d" % x)
+
+        if marks:
+            cp(T.lnu[:], T.PX0[:, 0:32], "PX00", "lnu")
+            act(T.MS[:], T.mk[:, 0:LN].indirect(T.lnu[:]), AF.Copy, "mk0 mk1 lnu", "MS")
+            send(T["lM%d" % t][:], T.MS[:], "M", t, "MS")
+        ts(T.cmu[:], T.PX0[:, 512:544], 2048.0, O.add, "PX01", "cmu")
+        act(T.Lg[:], T.TL[:, 0:Wt[0]].indirect(T.cmu[:]), AF.Copy, TLR + " cmu", "Lg")
+        send(T["lL%d" % t][:], T.Lg[:], "L", t, "Lg")
+        ts(T.lnf[:], T.PX0[:, 0:32], 0.0, O.add, "PX00", "lnf")
+        dups(0)
+        wb = slice(W0 + B * t, W0 + B * (t + 1))
+        wf = slice(TW + W0 + B * t, TW + W0 + B * (t + 1))
+        if not last:
+            act(T.TS[:, wb], T.TS[:, 0:Wt[0]].indirect(cu[:, 0:16]), AF.Copy, TSR + " cu0", "TS")
+            act(T.TL[:, wb], T.TL[:, 0:Wt[0]].indirect(cu[:, 0:16]), AF.Copy, TLR + " cu0", "TL")
+            ts(T.kh[:, 32:48], T.Yl[:, 0:16], -1.0, O.mult, "Yl", "kh2")
+            spread(T.PU, 0, 256, T.D15, T.kh, 32, "D15 kh2", "PU0")
+            act(T.TS[:, wf], T.PU[:, 0:256], AF.Copy, "PU0", "TS")
+            tt(T.uw[:], T.uf[:], T["wr%d" % t][:], O.mult, "uf wr%d" % t, "uw")
+        v_(lambda: V.tensor_scalar(T.rr[:], T.TC[:, 0:Wt[0]].indirect(cu[:, 0:16]), 0.5, 0.25, O.mult, O.add), TCR + " cu0", "rr")
+        firsts(0)
+        dups(1)
+        offs(0)
+        tt(T.r2[:], T.rr[:], T.fr[:, 0:256], O.mult, "rr fr0", "r2")
+        firsts(1)
+        if not last:
+            vlist(t + 1)
+        ts(T.TC[:, wb], T.r2[:], -D, O.add, "r2", "TC")
+        tt(T.aC[:], T.TC[:].indirect(T.ou[:, 0:16]), T.nu[:], O.mult, TCR + " ou0 nu", "aC")
+        tt(T.TC[:].indirect(T.ou[:, 0:16]), T.aC[:], T.u1[:], O.add, "aC u1 ou0", "TC")
+        offs(1)
+        if not last:
+            tt(T.aS[:], T.TS[:, 0:TW].indirect(T.ou[:, 0:16]), T.nu[:], O.mult, TSR + " ou0 nu", "aS")
+            tt(T.TS[:, 0:TW].indirect(T.ou[:, 0:16]), T.aS[:], T.uw[:], O.add, "aS uw ou0", "TS")
+        tt(T.aC[:], T.TC[:].indirect(T.ou[:, 16:32]), T.uf[:], O.add, TCR + " ou1 uf", "aC")
+        ts(T.aC[:], T.aC[:], 15.0 - D, O.min, "aC", "aC")
+        cp(T.TC[:].indirect(T.ou[:, 16:32]), T.aC[:], "aC ou1", "TC")
+        Wt[0] += B
+        if last:
+            for k in range(4):
+                for b in (0, 1):
+                    o = slice(1024 * k + 512 * b, 1024 * k + 512 * b + 512)
+                    if b or k == 3:
+                        act(T.yb[:, o], T.TC[:, o], AF.Relu, TCR, "yb%d%d" % (k, b))
+                    else:
+                        ts(T.yb[:, o], T.TC[:, o], 0.0, O.max, TCR, "yb%d%d" % (k, b))
+                o = slice(1024 * k, 1024 * k + 1024)
+                dma("S", T.yn[:, o], T.yb[:, o], "yb%d0 yb%d1" % (k, k), "yn%d" % k)
+        tt(T.tot[:, 1:2], T.tot[:, 0:1], T["lT%d" % t][:, 0:1], O.min, "tot lT%d" % t, "tm1")
+        tt(T.so[:], T.lnf[:], T.Dm[:], O.subtract, "lnf Dm", "so")
+        ts(T.tot[:, 2:3], T.tot[:, 1:2], float(CAP), O.min, "tm1", "tm2", 128.0, O.add)
+        tm = T.tot[:, 2:3]
+        ts(T.vd[:], T.mL[:], tm, O.is_le, "mL tm2", "vd")
+        ts(T.mvv[:], T.X[:], tm, O.is_le, "X tm2", "mvv")
+        tt(T.so[:], T.so[:], T.vd[:], O.mult, "so vd", "so")
+        tt(T.mvv[:], T.mvv[:], T.eb[:], O.mult, "mvv eb", "mvv")
+        tt(T.so[:], T.so[:], T.Dm[:], O.add, "so Dm", "so")
+        ts(T.nmv[:], T.mvv[:], -1.0, O.mult, "mvv", "nmv", 1.0, O.add)
+        cp(T.sou[:], T.so[:], "so", "sou")
+        tt(cf[:], cf[:], T.nmv[:], O.mult, "cf0 cf1 nmv", "cf0 cf1")
+        if not last:
+            tt(sm(0), sm(0), T.nmv[:, 0:16], O.mult, "F1 nmv", "F1")
+        cp(T.H[:].indirect(T.sou[:]), T["lL%d" % t][:], "sou lL%d" % t, "H")
+        listsum(T.PX0[:, 0:128], T.EH, T.H, 0, LN, "EH H", "PX00")
+        if marks:
+            cp(T.mk[:].indirect(T.sou[:]), T["lM%d" % t][:], "sou lM%d" % t, "mk0 mk1")
+        tt(cf[:], cf[:], T.PX0[:, 0:128], O.add, "cf0 cf1 PX00", "cf0 cf1")
+        if not last:
+            cp(cu[:], cf[:], "cf0 cf1", "cu0 cu1")
+            ts(nz[:], cf[:], 0.5, O.is_gt, "cf0 cf1", "nz0 nz1", float(TW), O.mult)
+    dma("A", T.yc[:, :], cf[:], "cf0 cf1", "yc")
+    for s in sorted(left):
+        if seen["G"].get(s, 0) < left[s]:
+            g.wait_ge(T.sem[s], left[s])

@@ -12,14 +12,15 @@ def _sb(dtype, **shapes):
 
 
 SCRATCH = {}
-SCRATCH.update(_sb("int32", tk=W0, ti0=CH, ti1=CH, ip=128, im=128, pg=128, mg=128, pm=128, mm=128, io3=-16, sfi=208, lki=208, lkj=208, cxi=128, rr=256))
+SCRATCH.update(_sb("int32", tk=W0, ti0=CH // 2, ti1=CH // 2, ip=128, im=128, pg=128, mg=128, pm=128, mm=128, io3=-16, sfi=208, lki=208, lkj=208,
+                   cxi=128, rr=256))
 SCRATCH.update(_sb("float32", TC=TW, TS=2 * TW, TL=4096, vl=384, Sg=LN, MK=640, sm=176, RS=16, RSn=16, dif=128, mrow=512, krow=128,
                    mi=32, mL=32, Dm=32, wr0=256, wr1=256, wr2=256, zz=128, cols=16, sff=208, lhf=208, llf=208, cf=128, nz=128, c2f=128,
                    xx=128, es=128, x2=128, o1=32, o2=32, uf=256, nu=256, u1=256, uw=256, r2=256, aC=256, aS=256,
                    inc=128, X=128, ha=128, hb=128, hc=128, Yl=128, lnf=32, tot=8, lT0=8, lT1=8, lT2=8, vd=32, so=32, mvv=128, nmv=128))
-SCRATCH.update(_sb("bfloat16", vvr=SP * LN, G=LN, cm=LN, mk=LN + CAP, H=LN + CAP, EQ=-256, yb=4096, ES=-128, Dn=-128, D15=-128, EV=-128, EW=-128,
-                   EH=-128, BO=128, PRE=128, ZT=128, DL=128, BN=128, B15=128, cc=640, tri=-16, eb=128, cr=512, fr=512, OH=512, MS=512, Lg=512,
-                   lM0=512, lM1=512, lL0=512, lL1=512, lL2=512))
+SCRATCH.update(_sb("bfloat16", vvr=SP * LN, G=LN, cm=LN, mk=LN + CAP, H=LN + CAP, EQ0=-256, EQ1=-256, BC=-128, yb=4096, ES=-128, Dn=-128, D15=-128,
+                   EV=-128, EW=-128, EH=-128, BO=128, PRE=128, ZT=128, NI=128, DL=128, BN=128, B15=128, cc=640, tri=-16, eb=128, cr=256, fr=512,
+                   OH=512, MS=512, Lg=512, lM0=512, lM1=512, lL0=512, lL1=512, lL2=512))
 SCRATCH.update(_sb("float16", q=LN, Y=LN, th=128, mmB=128, mm1=128, mmV=128, mv1=128, kh=64, R=512, off=128, kr=512, CG=512))
 SCRATCH.update(_sb("uint16", cu=128, cu2=128, ou=32, ofu=8, klu=32, cmu=32, lnu=32, sou=32))
 SCRATCH.update({k: ("psum", [128, n], "float32") for k, n in (("PX0", 1024), ("PX1", 1024), ("PU", 1024), ("PL0", 512), ("PL1", 512))})
@@ -129,6 +130,9 @@ def rank_program(g, core, T, topo):
                 wr["l%s%d" % (a, t)] = {"a%s%d" % (a, t): ne}
                 left["a%s%d" % (a, t)] = ne
 
+    def marks(t, s):
+        return not (t == RO - 1 and s == SP - 1)
+
     def sm(k):
         return T.sm[:, 16 * k:16 * k + 16]
 
@@ -205,36 +209,38 @@ def rank_program(g, core, T, topo):
     dma("S", T.TS[15:128:16, TW:TW + W0], T.sff[:], "sff TSF0 TSF1", "TSF")
     vlist(0)
     tt(cc(4), T.ip[:], T.im[:], O.is_le, "ip im", "c4")
-    tt(T.dif[:], T.im[:], T.ip[:], O.subtract, "im ip", "dif")
     tt(T.PRE[:], T.BO[:], cc(4), O.mult, "BO c4", "PRE")
-    ts(cc(0), T.dif[:], 1.0, O.is_equal, "dif", "c0")
-    ts(cc(1), T.dif[:], -15.0, O.is_equal, "dif", "c1")
     tt(T.ZT[:], T.PRE[:], T.BO[:], O.subtract, "PRE BO", "ZT")
-    ts(cc(2), T.dif[:], 0.0, O.is_equal, "dif", "c2")
-    tt(cc(0), cc(0), cc(1), O.add, "c0 c1", "c0")
-    ts(cc(3), T.mm[:], 15.0, O.is_lt, "mm", "c3")
-    tt(cc(0), cc(0), T.BO[:], O.mult, "c0 BO", "c0")
-    tt(cc(2), cc(2), cc(3), O.mult, "c2 c3", "c2")
-    ts(T.BN[:], T.BO[:], T.RS[:, 15:16], O.mult, "BO RS", "BN", 1024.0, O.mult)
-    tt(T.DL[:], cc(0), cc(2), O.subtract, "c0 c2", "DL")
-    ts(T.cols[:, 0:1], T.RS[:, 15:16], 800.0, O.mult, "RS", "cl0", -400.0, O.add)
-    ts(T.cols[:, 1:2], T.RS[:, 15:16], 1609800.0, O.mult, "RS", "cl1", -409800.0, O.add)
-    ts(T.cols[:, 2:3], T.pm[:, 0:1], 0.0, O.add, "pm", "cl2")
-    ts(T.cols[:, 3:4], T.RS[:, 0:1], 64.0, O.mult, "RS", "cl3a")
-    tt(T.cols[:, 4:5], T.cols[:, 3:4], T.RS[:, 1:2], O.add, "cl3a RS", "cl3")
-    for k in range(NCH):
-        sl = slice(k * CH, (k + 1) * CH)
+    for k in range(2 * NCH):
+        sl = slice(k * CH // 2, (k + 1) * CH // 2)
         ti, tn = T["ti%d" % (k % 2)], "ti%d" % (k % 2)
-        ts(ti[:], T.tk[:, sl], 15, O.bitwise_and, "tk%d" % k, tn)
-        ts(T.TC[:, sl], ti[:], -D, O.add, tn, "TC_%d" % k)
+        ts(ti[:], T.tk[:, sl], 15, O.bitwise_and, "tk%d" % (k // 2), tn)
+        ts(T.TC[:, sl], ti[:], -D, O.add, tn, "TC_%d" % (k // 2))
 
     def tables2():
         for k in range(NCH):
             sl = slice(k * CH, (k + 1) * CH)
             ts(T.TS[:, sl], T.tk[:, sl], -7.5, O.add, "tk%d" % k, "TS_%d" % k, MAG, O.add)
             act(T.TS[:, sl], T.TS[:, sl], AF.Identity, "TS_%d" % k, "TS_%d" % k, bias=-(MAG / 16) - 2048.0, scale=1.0 / 16)
-    tables2()
     v_(lambda: V.memset(sm(0), 0.0), "", "F1")
+
+    def consts2():
+        tt(T.dif[:], T.im[:], T.ip[:], O.subtract, "im ip", "dif")
+        ts(T.cols[:, 0:1], T.RS[:, 15:16], 800.0, O.mult, "RS", "cl0", -400.0, O.add)
+        ts(T.cols[:, 1:2], T.RS[:, 15:16], 1609800.0, O.mult, "RS", "cl1", -409800.0, O.add)
+        ts(cc(0), T.dif[:], 1.0, O.is_equal, "dif", "c0")
+        ts(cc(1), T.dif[:], -15.0, O.is_equal, "dif", "c1")
+        ts(cc(2), T.dif[:], 0.0, O.is_equal, "dif", "c2")
+        tt(cc(0), cc(0), cc(1), O.add, "c0 c1", "c0")
+        ts(cc(3), T.mm[:], 15.0, O.is_lt, "mm", "c3")
+        tt(cc(0), cc(0), T.BO[:], O.mult, "c0 BO", "c0")
+        tt(cc(2), cc(2), cc(3), O.mult, "c2 c3", "c2")
+        ts(T.BN[:], T.BO[:], T.RS[:, 15:16], O.mult, "BO RS", "BN", 1024.0, O.mult)
+        tt(T.DL[:], cc(0), cc(2), O.subtract, "c0 c2", "DL")
+        ts(T.NI[:], T.dif[:], 0.0, O.is_equal, "dif", "NI", -1.0, O.mult)
+        ts(T.cols[:, 2:3], T.pm[:, 0:1], 0.0, O.add, "pm", "cl2")
+        ts(T.cols[:, 3:4], T.RS[:, 0:1], 64.0, O.mult, "RS", "cl3a")
+        tt(T.cols[:, 4:5], T.cols[:, 3:4], T.RS[:, 1:2], O.add, "cl3a RS", "cl3")
 
     def late():
         v_(lambda: V.memset(T.zz[:], 0.0), "", "zz")
@@ -256,8 +262,6 @@ def rank_program(g, core, T, topo):
         ts(T.Dm[:], T.mL[:], float(LN - 129), O.add, "mL", "Dm")
         ts(sm(9), T.mL[:, 0:16], float(4096 - 129 - 2047), O.add, "mL", "bz")
         ts(sm(10), sm(9), 2047.0, O.add, "bz", "bz16", 16.0, O.mult)
-
-    def late_a():
         for i in range(16):
             act(T.D15[:, i, :], T.B15[:], AF.Copy, "B15 RSn", "D15%d" % i, scale=T.RSn[:, i:i + 1])
         wr["D15"] = wr["D1515"]
@@ -284,30 +288,38 @@ def rank_program(g, core, T, topo):
         else:
             tt(T.q[:, HL(h)], win, T.mk[:, HL(h)], O.mult, TCR + K(" cu@ mk@", h), K("q@", h))
 
+    def S2(h):
+        act(T.G[:, HL(h)], T.q[:, HL(h)], AF.Sigmoid, K("q@", h), K("G@", h), bias=-200.0, scale=400.0)
+
     def S3q(h):
         listsum(PL[h][:, 0:64], T.ES, T.q, 1024 * h, 1024 * h + 1024, K("q@ ES", h), K("PL@", h))
+        listsum(PL[h][:, 64:128], T.ES, T.q, 1024 * h, 1024 * h + 1024, K("q@ ES", h), K("PL@", h), stop=False)
 
+    def S3G(h):
+        listsum(PL[h][:, 64:128], T.ES, T.G, 1024 * h, 1024 * h + 1024, K("G@ ES", h), K("PL@", h), start=False)
+
+    def S3p(h):
         def f():
             for b in (0, 512):
                 x = P.matmul(PX[h][:, b:b + 512], T.PRE[:], T.q[:, 1024 * h + b:1024 * h + b + 512], True, False)
             return x
         p_(f, K("q@ PRE", h), K("PX@0 PX@1", h))
-        listsum(PL[h][:, 64:128], T.ES, T.q, 1024 * h, 1024 * h + 1024, K("q@ ES", h), K("PL@", h), stop=False)
 
-    def S2(h):
-        act(T.G[:, HL(h)], T.q[:, HL(h)], AF.Sigmoid, K("q@", h), K("G@", h), bias=-200.0, scale=400.0)
-
-    def S3G(h):
-        listsum(PL[h][:, 64:128], T.ES, T.G, 1024 * h, 1024 * h + 1024, K("G@ ES", h), K("PL@", h), start=False)
-
-    def S4(h, s):
+    def S4(h, s, o=None):
         C = HC(h)
+        fill = [] if o is None else S11(o)
         tt(T.xx[:, C], PL[h][:, 64:128], T.vl[:, 128 * s + 64 * h:128 * s + 64 * h + 64], O.mult, K("PL@ vl", h), K("xx@", h))
         tt(T.es[:, C], PL[h][:, 0:64], T.xx[:, C], O.is_le, K("PL@ xx@", h), K("es@", h))
+        for f in fill[0:1]:
+            f()
         tt(T.es[:, C], T.es[:, C], nz[:, C], O.mult, K("es@ nz@", h), K("es@", h))
+        for f in fill[1:2]:
+            f()
         tt(T.c2f[:, C], cf[:, C], T.es[:, C], O.add, K("cf@ es@", h), K("c2f@", h))
         tt(T.x2[:, C], T.xx[:, C], T.es[:, C], O.add, K("xx@ es@", h), K("x2@", h))
         cp(T.cu2[:, C], T.c2f[:, C], K("c2f@", h), K("cu2@", h))
+        for f in fill[2:3]:
+            f()
         ts(T.th[:, C], T.x2[:, C], 1025.0 - 0.4975, O.add, K("x2@", h), K("th@", h))
 
     def flist(s):
@@ -317,15 +329,14 @@ def rank_program(g, core, T, topo):
         tt(sm(3), sm(2), sm(1), O.mult, "t1 d1", "t2")
         tt(sm(4), sm(0), sm(3), O.add, "F1 t2", "Fo")
         if s == SP - 1:
-            tt(sm(2), sm(0), sm(5), O.mult, "F1 e01", "t1")
-            tt(sm(3), sm(0), sm(2), O.subtract, "F1 t1", "t2")
-            ts(sm(6), sm(3), 0.5, O.is_gt, "t2", "ca")
-            ts(sm(7), sm(3), -2048.0, O.add, "t2", "kf")
-            tt(sm(2), sm(1), sm(6), O.mult, "d1 ca", "t1")
-            ts(T.kh[:, 0:16], sm(7), -1.0, O.mult, "kf", "kh0")
-            ts(sm(8), sm(2), -2048.0, O.add, "t1", "kd")
-            ts(T.kh[:, 16:32], sm(8), -1.0, O.mult, "kd", "kh1")
+            tt(sm(2), sm(0), sm(5), O.is_gt, "F1 e01", "t1")
+            tt(sm(6), sm(2), sm(5), O.subtract, "t1 e01", "t2")
+            ts(sm(6), sm(6), 0.5, O.is_gt, "t2", "ca t2")
+            ts(T.kh[:, 32:48], sm(6), -1.0, O.mult, "ca", "kh2")
         tt(sm(0), sm(4), sm(5), O.mult, "Fo e01", "F1")
+        if s == SP - 2:
+            ts(sm(7), sm(0), -2048.0, O.add, "F1", "kf")
+            ts(T.kh[:, 0:16], sm(7), -1.0, O.mult, "kf", "kh0")
 
     def S5(h):
         act(T.Sg[:, HL(h)], T.TS[:, 0:TW + Wt[0]].indirect(T.cu2[:, HC(h)]), AF.Copy, TSR + K(" cu2@", h), K("Sg@", h))
@@ -335,16 +346,20 @@ def rank_program(g, core, T, topo):
             spread(PX[h], 512 * b, 512, T.Dn, T.th, 64 * h + 32 * b, K("th@ Dn", h), K("PX@%d" % b, h), start=False)
 
     def S7(h):
-        act(T.cm[:, HL(h)], PX[h][:], AF.Sigmoid, K("PX@0 PX@1 cl0 cl1", h), K("cm@", h), bias=T.cols[:, 1:2], scale=T.cols[:, 0:1])
+        for b in (0, 1):
+            act(T.cm[:, 1024 * h + 512 * b:1024 * h + 512 * b + 512], PX[h][:, 512 * b:512 * b + 512], AF.Sigmoid, K("PX@%d cl0 cl1" % b, h),
+                K("cm@%d" % b, h), bias=T.cols[:, 1:2], scale=T.cols[:, 0:1])
 
-    def P8(h, marks):
-        def f(ps, lhs):
-            for b in (0, 512):
-                x = P.matmul(ps[:, b:b + 512], lhs[:], T.cm[:, 1024 * h + b:1024 * h + b + 512], True, True)
-            return x
-        p_(lambda: f(T.PU, T.DL), K("cm@ DL", h), "PU0 PU1")
-        if marks:
-            p_(lambda: f(PX[h], T.BN), K("cm@ BN", h), K("PX@0 PX@1", h))
+    def P8(h, ps, lhs, r, w):
+        for b in (0, 1):
+            p_(lambda: P.matmul(ps[:, 512 * b:512 * b + 512], lhs[:], T.cm[:, 1024 * h + 512 * b:1024 * h + 512 * b + 512], True, True),
+               K(r % b, h), K(w % b, h))
+
+    def P8u(h):
+        P8(h, T.PU, T.DL, "cm@%d DL", "PU%d")
+
+    def P8t(h):
+        P8(h, PX[h], T.BN, "cm@%d BN", "PX@%d")
 
     def S9(h, s):
         tt(T.Y[:, HL(h)], T.Sg[:, HL(h)], T.PU[:], O.mult, K("Sg@ PU0 PU1", h), K("Y@", h))
@@ -359,59 +374,109 @@ def rank_program(g, core, T, topo):
 
     def S11(h):
         C, y = HC(h), PL[h][:, 128:192]
-        ts(cu[:, C], y, 2048.0, O.add, K("PL@", h), K("cu@", h))
-        ts(cf[:, C], y, 2048.0, O.add, K("PL@", h), K("cf@", h))
-        ts(nz[:, C], y, -2047.5, O.is_gt, K("PL@", h), K("nz@", h), float(TW), O.mult)
+        return [lambda: ts(cu[:, C], y, 2048.0, O.add, K("PL@", h), K("cu@", h)),
+                lambda: ts(cf[:, C], y, 2048.0, O.add, K("PL@", h), K("cf@", h)),
+                lambda: ts(nz[:, C], y, -2047.5, O.is_gt, K("PL@", h), K("nz@", h), float(TW), O.mult)]
+
+    def eqs(x):
+        def one(k):
+            return lambda: ts(T["EQ%d" % x][:, k, 0:256 - 16 * k], T.R[:, 256 * x + 16 * k:256 * x + 256], T.sm[:, 112 + 16 * x + k:113 + 16 * x + k],
+                              O.is_equal, "R%d %s" % (x, ("kf", "kd")[x]), "E%d_%d" % (x, k))
+        alle = " ".join("E%d_%d" % (x, k) for k in range(16))
+        d = T["EQ%d" % x][:, :, 0:16]
+        return [one(k) for k in range(16)] + [lambda: tt(d, d, T.tri[:], O.mult, alle + " tri", alle)]
+
+    def rows(c, kn, ps, base, key):
+        spread(ps, base, 256, T.Dn, T.kh, c, "Dn " + kn, key)
+
+    def slot(h, t, s, o, so):
+        keyf, keyd, cand = h == 1 and s == SP - 2, h == 0 and s == SP - 1, h == 1 and s == SP - 1
+        eq = eqs(0)[0:9] if keyd else eqs(0)[9:] if cand else []
+        S1(h, t, s)
+        if o is not None:
+            P8u(o)
+        S2(h)
+        S3q(h)
+        if keyd:
+            ts(sm(8), cf[:, 0:16], 1.0 - 2048.0, O.add, "cf0", "kd")
+            ts(T.kh[:, 16:32], sm(8), -1.0, O.mult, "kd", "kh1")
+        for f in eq[0:2]:
+            f()
+        if o is not None:
+            S9(o, so)
+        if h == 1:
+            flist(s)
+        else:
+            for f in eq[2:]:
+                f()
+        S3G(h)
+        if o is not None:
+            S10(o)
+            if marks(t, so):
+                P8t(o)
+        S3p(h)
+        if keyf:
+            rows(0, "kh0", T.PU, 0, "PU0")
+        if keyd:
+            rows(16, "kh1", T.PU, 0, "PU0")
+        if t == s == 0 and h == 0:
+            tables2()
+        S4(h, s, o)
+        P6(h)
+        if cand:
+            rows(32, "kh2", T.PL0, 256, "PL0")
+        S5(h)
+        if cand:
+            act(T.cr[:], T.PL0[:, 256:512], AF.Copy, "PL0", "cr")
+        if t == s == 0 and h == 0:
+            consts2()
+        if keyf:
+            cp(T.R[:, 0:256], T.PU[:, 0:256], "PU0", "R0")
+        if keyd:
+            cp(T.R[:, 256:512], T.PU[:, 0:256], "PU0", "R1")
+        if o is not None and marks(t, so):
+            M(o)
+        S7(h)
+        if cand:
+            for f in eq[2:]:
+                f()
+            for k in range(16):
+                act(T.BC[:, k, :], T.BO[:], AF.Copy, "BO ca", "BC%d" % k, scale=T.sm[:, 96 + k:97 + k])
+
+    def dups(x):
+        def f():
+            for k in range(16):
+                y = P.matmul(PL[x][:, 256 + 16 * k:512], T.BC[:, k, :], T["EQ%d" % x][:, k, 0:256 - 16 * k], k == 0, k == 15)
+            return y
+        p_(f, " ".join("E%d_%d BC%d" % (x, k, k) for k in range(16)), "PL%d" % x)
+
+    def firsts(x):
+        sl = slice(256 * x, 256 * x + 256)
+        tt(T.fr[:, sl], PL[x][:, 256:512], T.cr[:], O.is_lt, "PL%d cr" % x, "fr%d" % x)
+        listsum(PL[x][:, 192:208], T.ES, T.fr, 256 * x, 256 * x + 256, "fr%d ES" % x, "PL%d" % x)
+
+    def offs(x):
+        kk, o, kn = 7 + x, slice(16 * x, 16 * x + 16), ("kf", "kd")[x]
+        tt(T.o1[:, o], sm(kk), sm(9), O.subtract, kn + " bz", "o1%d" % x)
+        tt(T.o2[:, o], T.o1[:, o], PL[x][:, 192:208], O.mult, "o1%d PL%d" % (x, x), "o2%d" % x)
+        tt(T.o1[:, o], T.o2[:, o], sm(10), O.add, "o2%d bz16" % x, "o1%d" % x)
+        ts(T.ou[:, o], T.o1[:, o], 1.0 / 16, O.mult, "o1%d" % x, "ou%d" % x)
 
     for t in range(RO):
         last = t == RO - 1
         iota(T.MK[:], [[0, 640]], 0, 0, "MK")
         iota(T.H[:, 0:LN], [[0, LN]], 0, 0, "H")
         for s in range(SP):
-            marks = not (last and s == SP - 1)
-            S1(0, t, s)
-            S3q(0)
-            if s:
-                S9(1, s - 1)
-                S10(1)
-                M(1)
-            S2(0)
-            S3G(0)
-            if s:
-                S11(1)
-            S4(0, s)
-            S5(0)
-            P6(0)
-            S7(0)
-            P8(0, marks)
-            S1(1, t, s)
-            S3q(1)
-            flist(s)
-            if t == 0 and s == 0:
+            slot(0, t, s, 1 if s else None, s - 1)
+            slot(1, t, s, 0, s)
+            if t == s == 0:
                 late()
-            S9(0, s)
-            S10(0)
-            if marks:
-                M(0)
-            S2(1)
-            S3G(1)
-            S11(0)
-            S4(1, s)
-            S5(1)
-            P6(1)
-            S7(1)
-            if s < SP - 1:
-                P8(1, marks)
-            if t == 0 and s == 0:
-                late_a()
         if not last:
             loadv("S", t + 1)
         tot = T.PX0[:, 0:128]
         ts(T.eb[:], T.es[:], 0.5, O.is_gt, "es0 es1", "eb")
         p_(lambda: P.matmul(tot, T.BO[:], T.eb[:], True, True), "BO eb", "PX00")
         p_(lambda: P.matmul(T.PX0[:, 512:640], T.ZT[:], T.eb[:], True, True), "ZT eb", "PX01")
-        spread(T.PL0, 256, 256, T.Dn, T.kh, 0, "Dn kh0", "PL0")
-        spread(T.PL1, 256, 256, T.Dn, T.kh, 16, "Dn kh1", "PL1")
         v_(lambda: V.tensor_tensor_scan(T.inc[:], tot, T.zz[:], 128.0, O.add, O.add), "PX00 zz", "inc")
         ts(T.hc[:], tot, 0.5, O.is_gt, "PX00", "hc")
         tt(T.ha[:], T.inc[:], tot, O.subtract, "inc PX00", "ha")
@@ -421,27 +486,44 @@ def rank_program(g, core, T, topo):
         tt(T.ha[:], T.ha[:], T.hb[:], O.mult, "ha hb", "ha")
         tt(T.off[:], T.ha[:], T.krow[:], O.max, "ha krow", "off")
         listsum(T.PX0[:, 0:8], T.ES, T.off, 0, 128, "off ES", "PX00")
-        P8(1, marks)
+        P8u(1)
+        if not last:
+            def f():
+                for b in (0, 512):
+                    P.matmul(T.PX1[:, b:b + 512], T.NI[:], T.q[:, 1024 + b:1536 + b], True, False)
+                    x = P.matmul(T.PX1[:, b:b + 512], T.BN[:], T.cm[:, 1024 + b:1536 + b], False, True)
+                return x
+            p_(f, "q1 cm10 cm11 NI BN", "PX10 PX11")
         ts(T.tot[:, 0:1], T.inc[:, 127:128], -128.0, O.add, "inc", "tot")
         send(T["lT%d" % t][:, 0:1], T.tot[:, 0:1], "T", t, "tot")
         tt(T.X[:], T.X[:], T.eb[:], O.mult, "X eb", "X")
-        cp(T.R[:, 0:256], T.PL0[:, 256:512], "PL0", "R0")
+        eq = eqs(1)
+        for f in eq[0:4]:
+            f()
         ts(T.ofu[:], T.PX0[:, 0:8], 1.0 / 16, O.mult, "PX00", "ofu")
         cp(T.MK[:, 0:640].indirect(T.ofu[:]), T.krow[:], "krow ofu", "MK")
-        cp(T.R[:, 256:512], T.PL1[:, 256:512], "PL1", "R1")
+        for f in eq[4:6]:
+            f()
         v_(lambda: V.tensor_tensor_scan(T.kr[:], T.MK[:, 128:640], T.MK[:, 128:640], 0.0, O.max, O.max), "MK", "kr")
         S9(1, SP - 1)
         S10(1)
         listsum(T.PX0[:, 0:32], T.ES, T.kr, 0, 512, "kr ES", "PX00")
-        if marks:
-            M(1)
-        ts(T.nu[:], T.uf[:], -1.0, O.mult, "uf", "nu", 1.0, O.add)
-        S11(1)
+        dups(0)
+        for f in eq[6:12]:
+            f()
+        if not last:
+            act(T.mk[:, HL(1)], T.PX1[:], AF.Sigmoid, "PX10 PX11", "mk1", bias=-200.0, scale=400.0 / D)
+        act(T.nu[:], T.uf[:], AF.Identity, "uf", "nu", bias=1.0, scale=-1.0)
+        act(T.u1[:], T.uf[:], AF.Copy, "uf", "u1", scale=1.0 - D)
+        for f in S11(1):
+            f()
         ts(T.klu[:], T.PX0[:, 0:32], 1.0 / 16, O.mult, "PX00", "klu")
         ts(T.Yl[:], cf[:], -2048.0, O.add, "cf0 cf1", "Yl")
         tt(T.OH[:], T.X[:].indirect(T.klu[:]), T.mrow[:], O.is_equal, "X klu mrow", "OH")
         tt(T.CG[:], T.Yl[:].indirect(T.klu[:]), T.OH[:], O.mult, "Yl klu OH", "CG")
-        if marks:
+        for f in eq[12:]:
+            f()
+        if not last:
             listsum(T.PX0[:, 0:32], T.ES, T.kr, 0, 512, "kr ES", "PX00", stop=False)
             listsum(T.PX0[:, 0:32], T.EW, T.OH, 0, 512, "OH EW", "PX00", start=False)
             listsum(T.PX0[:, 512:544], T.ES, T.CG, 0, 512, "CG ES", "PX01")
@@ -449,64 +531,35 @@ def rank_program(g, core, T, topo):
             listsum(T.PX0[:, 512:544], T.ES, T.CG, 0, 512, "CG ES", "PX01")
             listsum(T.PX0[:, 0:32], T.ES, T.kr, 0, 512, "kr ES", "PX00", stop=False)
             listsum(T.PX0[:, 0:32], T.EW, T.OH, 0, 512, "OH EW", "PX00", start=False)
-        ts(T.u1[:], T.uf[:], 1.0 - D, O.mult, "uf", "u1")
-
-        def dups(x):
-            kk, R, kn = 112 + 16 * x, T.R, ("kf", "kd")[x]
-            for k in range(16):
-                ts(T.EQ[:, k, 0:256 - 16 * k], R[:, 256 * x + 16 * k:256 * x + 256], T.sm[:, kk + k:kk + k + 1], O.is_equal, "R%d %s" % (x, kn), "EQ%d" % k)
-            alle = " ".join("EQ%d" % k for k in range(16))
-            tt(T.EQ[:, :, 0:16], T.EQ[:, :, 0:16], T.tri[:], O.mult, alle + " tri", alle)
-
-            def f():
-                for k in range(16):
-                    y = P.matmul(PL[x][:, 256 + 16 * k:512], T.BO[:], T.EQ[:, k, 0:256 - 16 * k], k == 0, k == 15)
-                return y
-            p_(f, alle + " BO", "PL%d" % x)
-            ts(T.cr[:, 256 * x:256 * x + 256], R[:, 256 * x:256 * x + 256], -2047.5, O.is_gt, "R%d" % x, "cr%d" % x)
-
-        def firsts(x):
-            sl = slice(256 * x, 256 * x + 256)
-            tt(T.fr[:, sl], PL[x][:, 256:512], T.cr[:, sl], O.is_lt, "PL%d cr%d" % (x, x), "fr%d" % x)
-            listsum(PL[x][:, 192:208], T.ES, T.fr, 256 * x, 256 * x + 256, "fr%d ES" % x, "PL%d" % x)
-
-        def offs(x):
-            kk, o, kn = 7 + x, slice(16 * x, 16 * x + 16), ("kf", "kd")[x]
-            tt(T.o1[:, o], sm(kk), sm(9), O.subtract, kn + " bz", "o1%d" % x)
-            tt(T.o2[:, o], T.o1[:, o], PL[x][:, 192:208], O.mult, "o1%d PL%d" % (x, x), "o2%d" % x)
-            tt(T.o1[:, o], T.o2[:, o], sm(10), O.add, "o2%d bz16" % x, "o1%d" % x)
-            ts(T.ou[:, o], T.o1[:, o], 1.0 / 16, O.mult, "o1%d" % x, "ou%d" % x)
-
-        if marks:
+        firsts(0)
+        dups(1)
+        if not last:
             cp(T.lnu[:], T.PX0[:, 0:32], "PX00", "lnu")
             act(T.MS[:], T.mk[:, 0:LN].indirect(T.lnu[:]), AF.Copy, "mk0 mk1 lnu", "MS")
             send(T["lM%d" % t][:], T.MS[:], "M", t, "MS")
         ts(T.cmu[:], T.PX0[:, 512:544], 2048.0, O.add, "PX01", "cmu")
         act(T.Lg[:], T.TL[:, 0:Wt[0]].indirect(T.cmu[:]), AF.Copy, TLR + " cmu", "Lg")
         send(T["lL%d" % t][:], T.Lg[:], "L", t, "Lg")
-        ts(T.lnf[:], T.PX0[:, 0:32], 0.0, O.add, "PX00", "lnf")
-        dups(0)
+        offs(0)
+        firsts(1)
+        act(T.lnf[:], T.PX0[:, 0:32], AF.Copy, "PX00", "lnf")
         wb = slice(W0 + B * t, W0 + B * (t + 1))
         wf = slice(TW + W0 + B * t, TW + W0 + B * (t + 1))
         if not last:
             act(T.TS[:, wb], T.TS[:, 0:Wt[0]].indirect(cu[:, 0:16]), AF.Copy, TSR + " cu0", "TS")
             act(T.TL[:, wb], T.TL[:, 0:Wt[0]].indirect(cu[:, 0:16]), AF.Copy, TLR + " cu0", "TL")
-            ts(T.kh[:, 32:48], T.Yl[:, 0:16], -1.0, O.mult, "Yl", "kh2")
-            spread(T.PU, 0, 256, T.D15, T.kh, 32, "D15 kh2", "PU0")
+            ts(T.kh[:, 48:64], T.Yl[:, 0:16], -1.0, O.mult, "Yl", "kh3")
+            spread(T.PU, 0, 256, T.D15, T.kh, 48, "D15 kh3", "PU0")
             act(T.TS[:, wf], T.PU[:, 0:256], AF.Copy, "PU0", "TS")
             tt(T.uw[:], T.uf[:], T["wr%d" % t][:], O.mult, "uf wr%d" % t, "uw")
         v_(lambda: V.tensor_scalar(T.rr[:], T.TC[:, 0:Wt[0]].indirect(cu[:, 0:16]), 0.5, 0.25, O.mult, O.add), TCR + " cu0", "rr")
-        firsts(0)
-        dups(1)
-        offs(0)
+        offs(1)
         tt(T.r2[:], T.rr[:], T.fr[:, 0:256], O.mult, "rr fr0", "r2")
-        firsts(1)
         if not last:
             vlist(t + 1)
         ts(T.TC[:, wb], T.r2[:], -D, O.add, "r2", "TC")
         tt(T.aC[:], T.TC[:].indirect(T.ou[:, 0:16]), T.nu[:], O.mult, TCR + " ou0 nu", "aC")
         tt(T.TC[:].indirect(T.ou[:, 0:16]), T.aC[:], T.u1[:], O.add, "aC u1 ou0", "TC")
-        offs(1)
         if not last:
             tt(T.aS[:], T.TS[:, 0:TW].indirect(T.ou[:, 0:16]), T.nu[:], O.mult, TSR + " ou0 nu", "aS")
             tt(T.TS[:, 0:TW].indirect(T.ou[:, 0:16]), T.aS[:], T.uw[:], O.add, "aS uw ou0", "TS")
@@ -540,7 +593,7 @@ def rank_program(g, core, T, topo):
             tt(sm(0), sm(0), T.nmv[:, 0:16], O.mult, "F1 nmv", "F1")
         cp(T.H[:].indirect(T.sou[:]), T["lL%d" % t][:], "sou lL%d" % t, "H")
         listsum(T.PX0[:, 0:128], T.EH, T.H, 0, LN, "EH H", "PX00")
-        if marks:
+        if not last:
             cp(T.mk[:].indirect(T.sou[:]), T["lM%d" % t][:], "sou lM%d" % t, "mk0 mk1")
         tt(cf[:], cf[:], T.PX0[:, 0:128], O.add, "cf0 cf1 PX00", "cf0 cf1")
         if not last:

from concourse.mybir import AluOpType as O, ActivationFunctionType as AF

W0, B, LN, RO, SP, CAP = 3328, 256, 2048, 3, 3, 512
TW = 4352
D = 2.0 ** -14
MAG = 1.5 * 2.0 ** 27
NCH, CH = 4, 832


def _sb(dtype, **shapes):
    return {k: ("sbuf", [128] + ([n] if n > 0 else [16, -n]), dtype) for k, n in shapes.items()}


SCRATCH = {}
SCRATCH.update(_sb("int32", tk=W0, ti0=CH // 2, ti1=CH // 2, ip=128, im=128, pg=128, mg=128, pm=128, mm=128, io3=-16, sfi=208, lki=208, lkj=208,
                   cxi=128, rr=256))
SCRATCH.update(_sb("float32", TC=TW, TS=2 * TW, TL=4096, vl=384, Sg=LN, MK=640, sm=176, RS=16, RSn=16, dif=128, mrow=512, krow=128,
                   mi=32, mL=32, Dm=32, wr0=256, wr1=256, wr2=256, zz=128, cols=16, sff=208, lhf=208, llf=208, cf=128, nz=128, c2f=128,
                   xx=128, es=128, x2=128, o1=32, o2=32, uf=256, nu=256, u1=256, uw=256, r2=256, aC=256, aS=256,
                   inc=128, X=128, ha=128, hb=128, hc=128, Yl=128, lnf=32, tot=8, lT0=8, lT1=8, lT2=8, vd=32, so=32, mvv=128, nmv=128))
SCRATCH.update(_sb("bfloat16", vvr=SP * LN, G=LN, cm=LN, mk=LN + CAP, H=LN + CAP, EQ0=-256, EQ1=-256, BC=-128, yb=4096, ES=-128, Dn=-128, D15=-128,
                   EV=-128, EW=-128, EH=-128, BO=128, PRE=128, ZT=128, NI=128, DL=128, BN=128, B15=128, cc=640, tri=-16, eb=128, cr=256, fr=512,
                   OH=512, MS=512, Lg=512, lM0=512, lM1=512, lL0=512, lL1=512, lL2=512))
SCRATCH.update(_sb("float16", q=LN, Y=LN, th=128, mmB=128, mm1=128, mmV=128, mv1=128, kh=64, R=512, off=128, kr=512, CG=512))
SCRATCH.update(_sb("uint16", cu=128, cu2=128, ou=32, ofu=8, klu=32, cmu=32, lnu=32, sou=32))
SCRATCH.update({k: ("psum", [128, n], "float32") for k, n in (("PX0", 1024), ("PX1", 1024), ("PU", 1024), ("PL0", 512), ("PL1", 512))})
DMAS = ["d%d" % i for i in range(24)]
REM = [a + str(t) for t in range(RO) for a in ("aT", "aM", "aL", "nT", "nM", "nL") if not (t == RO - 1 and a[1] == "M")]
SEMAPHORES = ["sV", "sA", "sP", "sG"] + DMAS + REM
BANKS = {"PX00", "PX01", "PX10", "PX11", "PU0", "PU1", "PL0", "PL1"}


def rank_program(g, core, T, topo):
    rank = T.rank_of(core)
    if rank is None:
        return
    V, A, P, S = g.vector, g.scalar, g.tensor, g.sync
    eng = {"V": V, "A": A, "P": P, "S": S, "G": g}
    seen = {k: {} for k in eng}
    cnt = {k: 0 for k in "VAPG"}
    wr, rd, left = {}, {}, {}
    ndma = [0]

    def run(qn, fn, r, w, acc=False, sem=None, remote=False, n=1):
        r, w = r.split(), w.split()
        own = "s" + qn
        need = {}

        def want(toks, skip):
            for s, v in toks.items():
                if not (skip and s == own):
                    need[s] = max(need.get(s, 0), v)
        for k in r:
            want(wr.get(k, {}), False)
            if k in BANKS:
                want(rd.get(k, {}), True)
        for k in w:
            want(wr.get(k, {}), acc)
            want(rd.get(k, {}), sem is None)
        for s in sorted(need):
            if seen[qn].get(s, 0) < need[s]:
                eng[qn].wait_ge(T.sem[s], need[s])
                seen[qn][s] = need[s]
        inst = fn()
        if sem is None:
            cnt[qn] += 1
            s, v = own, cnt[qn]
        else:
            s, v = sem, n
        if not remote:
            inst.then_inc(T.sem[s], n)
        left[s] = v
        for k in r:
            rd.setdefault(k, {})[s] = v
        for k in w:
            wr[k] = {s: v}
            rd[k] = {}

    def v_(fn, r, w): run("V", fn, r, w)
    def a_(fn, r, w): run("A", fn, r, w)
    def p_(fn, r, w): run("P", fn, r, w, acc=True)
    def g_(fn, r, w): run("G", fn, r, w)

    def dma(qn, out, in_, r, w):
        s = DMAS[ndma[0]]
        ndma[0] += 1
        run(qn, lambda: eng[qn].dma_start(out, in_), r, w, sem=s, n=16)

    def ts(out, in0, s1, op0, r, w, s2=None, op1=None):
        if op1 is None:
            v_(lambda: V.tensor_scalar(out, in0, s1, None, op0), r, w)
        else:
            v_(lambda: V.tensor_scalar(out, in0, s1, s2, op0, op1), r, w)

    def tt(out, in0, in1, op, r, w):
        v_(lambda: V.tensor_tensor(out, in0, in1, op), r, w)

    def cp(out, in_, r, w):
        v_(lambda: V.tensor_copy(out, in_), r, w)

    def act(out, in_, func, r, w, bias=0.0, scale=1.0):
        a_(lambda: A.activation(out, in_, func, bias=bias, scale=scale), r, w)

    def listsum(out, fam, src, lo, hi, r, w, start=True, stop=True):
        def f():
            for i in range(16):
                x = P.matmul(out, fam[:, i, :], src[:, lo + i:hi:16], start and i == 0, stop and i == 15)
            return x
        p_(f, r, w)

    def spread(out, base, n, fam, src, lo, r, w, start=True):
        def f():
            for i in range(16):
                x = P.matmul(out[:, base + i:base + n:16], fam[:, i, :], src[:, lo:lo + n // 16], start, start or i == 15)
            return x
        p_(f, r, w)

    nxt = T.cores[(rank + 1) % len(T.cores)]
    rid, pid, _se = topo.addr(nxt)
    emask = topo.mask(core, nxt)
    ne = len(topo.engines(core, nxt))

    def send(dst, src, name, t, r):
        s, rs = "n%s%d" % (name, t), "a%s%d" % (name, t)
        run("G", lambda: g.remote_dma(dst, src, T.sem[rs], T.sem[s], pid, rid, emask), r, "", sem=s, remote=True, n=ne)

    for t in range(RO):
        for a in "TML":
            if t < RO - 1 or a != "M":
                wr["l%s%d" % (a, t)] = {"a%s%d" % (a, t): ne}
                left["a%s%d" % (a, t)] = ne

    def marks(t, s):
        return not (t == RO - 1 and s == SP - 1)

    def sm(k):
        return T.sm[:, 16 * k:16 * k + 16]

    def cc(k):
        return T.cc[:, 128 * k:128 * k + 128]

    def loadv(qn, t):
        dma(qn, T.vvr[0:8, :], T.vv[:, SP * LN * t:SP * LN * (t + 1)], "", "vvr")

    def vlist(t):
        for s in range(SP):
            def f(s=s):
                for i in range(16):
                    x = P.matmul(T.PU[:, 512 + 128 * s:640 + 128 * s], T.EV[0:8, i, :], T.vvr[0:8, LN * s + i:LN * (s + 1):16], i == 0, i == 15)
                return x
            p_(f, "EV vvr", "PU1")
        act(T.vl[:], T.PU[:, 512:512 + 128 * SP], AF.Copy, "PU1", "vl", scale=1.0 / 256)

    loadv("A", 0)
    for k in range(NCH):
        dma("S", T.tk[:, k * CH:(k + 1) * CH], T.tab[:, k * CH:(k + 1) * CH], "", "tk%d" % k)
        if k == 0:
            dma("S", T.cxi[:], T.cx[:, :], "", "cxi")
            dma("S", T.sfi[:], T.suf[:, :], "", "sfi")
    dma("S", T.lki[:], T.lnk[:, :], "", "lki")

    def iota(out, pat, base, cm, w, small=True):
        if small:
            g_(lambda: g.iota(out, pat, base, cm, allow_small_or_imprecise_dtypes=True), "", w)
        else:
            g_(lambda: g.iota(out, pat, base, cm), "", w)
    iota(T.ip[:], [[0, 128]], 0, 1, "ip", False)
    iota(T.im[:], [[1, 128]], 0, 0, "im", False)
    iota(T.TS[:, TW:TW + 2176], [[0, 2176]], 0, 0, "TSF0")
    iota(T.TS[:, TW + 2176:2 * TW], [[0, 2176]], 0, 0, "TSF1")
    iota(T.TC[:, W0:TW], [[0, TW - W0]], 0, 0, "TCz")
    iota(T.TS[:, W0:TW], [[0, TW - W0]], 0, 0, "TSz")
    iota(T.mi[:], [[16, 32]], 129, 0, "mi")
    iota(T.io3[:], [[0, 16], [1, 16]], 0, 0, "io3", False)
    iota(T.krow[:], [[1, 128]], 0, 0, "krow")
    iota(T.TL[:], [[0, 4096]], 0, 0, "TL")
    iota(T.mrow[:], [[1, 512]], 129, 0, "mrow")
    for t in range(RO):
        iota(T["wr%d" % t][:], [[1, 256]], W0 + B * t - 2048, 0, "wr%d" % t)
    iota(T.H[:, LN:], [[0, CAP]], 0, 0, "H")

    ts(T.pg[:], T.ip[:], 4, O.arith_shift_right, "ip", "pg")
    ts(T.mg[:], T.im[:], 4, O.arith_shift_right, "im", "mg")
    ts(T.pm[:], T.ip[:], 15, O.bitwise_and, "ip", "pm")
    ts(T.mm[:], T.im[:], 15, O.bitwise_and, "im", "mm")
    tt(T.BO[:], T.pg[:], T.mg[:], O.is_equal, "pg mg", "BO")
    tt(T.RS[:], T.pm[:, 0:16], T.mm[:, 0:16], O.is_equal, "pm mm", "RS")
    ts(T.mm1[:], T.mm[:], 1.0, O.add, "mm", "mm1")
    tt(T.mv1[:], T.mg[:], T.ip[:], O.is_equal, "mg ip", "mv1")
    ts(T.RSn[:], T.RS[:], -1.0, O.mult, "RS", "RSn")
    tt(T.mv1[:], T.mv1[:], T.mm1[:], O.mult, "mv1 mm1", "mv1")
    tt(T.mm1[:], T.mm1[:], T.BO[:], O.mult, "mm1 BO", "mm1")
    ts(T.mmV[:], T.mv1[:], -1.0, O.add, "mv1", "mmV")
    ts(T.mmB[:], T.mm1[:], -1.0, O.add, "mm1", "mmB")
    for i in range(16):
        ts(T.EV[0:8, i, :], T.mmV[0:8, :], float(i), O.is_equal, "mmV", "EV%d" % i)
    for i in range(16):
        ts(T.ES[:, i, :], T.mmB[:], float(i), O.is_equal, "mmB", "ES%d" % i)
    wr["EV"] = wr["EV15"]
    wr["ES"] = wr["ES15"]
    for i in range(16):
        act(T.Dn[:, i, :], T.BO[:], AF.Copy, "BO RSn", "Dn%d" % i, scale=T.RSn[:, i:i + 1])
    wr["Dn"] = wr["Dn15"]
    cu, cf, nz = T.cu, T.cf, T.nz
    cp(cu[:], T.cxi[:], "cxi", "cu0 cu1")
    cp(cf[:], T.cxi[:], "cxi", "cf0 cf1")
    ts(T.sff[:], T.sfi[:], -2048.0, O.add, "sfi", "sff")
    ts(nz[:], cf[:], 0.5, O.is_gt, "cf0 cf1", "nz0 nz1", float(TW), O.mult)
    dma("S", T.TS[15:128:16, TW:TW + W0], T.sff[:], "sff TSF0 TSF1", "TSF")
    vlist(0)
    tt(cc(4), T.ip[:], T.im[:], O.is_le, "ip im", "c4")
    tt(T.PRE[:], T.BO[:], cc(4), O.mult, "BO c4", "PRE")
    tt(T.ZT[:], T.PRE[:], T.BO[:], O.subtract, "PRE BO", "ZT")
    for k in range(2 * NCH):
        sl = slice(k * CH // 2, (k + 1) * CH // 2)
        ti, tn = T["ti%d" % (k % 2)], "ti%d" % (k % 2)
        ts(ti[:], T.tk[:, sl], 15, O.bitwise_and, "tk%d" % (k // 2), tn)
        ts(T.TC[:, sl], ti[:], -D, O.add, tn, "TC_%d" % (k // 2))

    def tables2():
        for k in range(NCH):
            sl = slice(k * CH, (k + 1) * CH)
            ts(T.TS[:, sl], T.tk[:, sl], -7.5, O.add, "tk%d" % k, "TS_%d" % k, MAG, O.add)
            act(T.TS[:, sl], T.TS[:, sl], AF.Identity, "TS_%d" % k, "TS_%d" % k, bias=-(MAG / 16) - 2048.0, scale=1.0 / 16)
    v_(lambda: V.memset(sm(0), 0.0), "", "F1")

    def consts2():
        tt(T.dif[:], T.im[:], T.ip[:], O.subtract, "im ip", "dif")
        ts(T.cols[:, 0:1], T.RS[:, 15:16], 800.0, O.mult, "RS", "cl0", -400.0, O.add)
        ts(T.cols[:, 1:2], T.RS[:, 15:16], 1609800.0, O.mult, "RS", "cl1", -409800.0, O.add)
        ts(cc(0), T.dif[:], 1.0, O.is_equal, "dif", "c0")
        ts(cc(1), T.dif[:], -15.0, O.is_equal, "dif", "c1")
        ts(cc(2), T.dif[:], 0.0, O.is_equal, "dif", "c2")
        tt(cc(0), cc(0), cc(1), O.add, "c0 c1", "c0")
        ts(cc(3), T.mm[:], 15.0, O.is_lt, "mm", "c3")
        tt(cc(0), cc(0), T.BO[:], O.mult, "c0 BO", "c0")
        tt(cc(2), cc(2), cc(3), O.mult, "c2 c3", "c2")
        ts(T.BN[:], T.BO[:], T.RS[:, 15:16], O.mult, "BO RS", "BN", 1024.0, O.mult)
        tt(T.DL[:], cc(0), cc(2), O.subtract, "c0 c2", "DL")
        ts(T.NI[:], T.dif[:], 0.0, O.is_equal, "dif", "NI", -1.0, O.mult)
        ts(T.cols[:, 2:3], T.pm[:, 0:1], 0.0, O.add, "pm", "cl2")
        ts(T.cols[:, 3:4], T.RS[:, 0:1], 64.0, O.mult, "RS", "cl3a")
        tt(T.cols[:, 4:5], T.cols[:, 3:4], T.RS[:, 1:2], O.add, "cl3a RS", "cl3")

    def late():
        v_(lambda: V.memset(T.zz[:], 0.0), "", "zz")
        ts(T.lkj[:], T.lki[:], 6, O.arith_shift_right, "lki", "lkj")
        ts(T.lki[:], T.lki[:], 63, O.bitwise_and, "lki", "lki")
        cp(T.lhf[:], T.lkj[:], "lkj", "lhf")
        cp(T.llf[:], T.lki[:], "lki", "llf")
        dma("S", T.TL[0:128:16, 0:W0], T.lhf[:], "lhf TL", "TLa")
        dma("S", T.TL[1:128:16, 0:W0], T.llf[:], "llf TL", "TLb")
        ts(cc(3), T.mm[:], 15.0, O.is_equal, "mm", "c3")
        ts(T.tri[:], T.io3[:], T.cols[:, 2:3], O.is_gt, "io3 cl2", "tri")
        tt(T.B15[:], T.BO[:], cc(3), O.mult, "BO c3", "B15")
        ts(T.mL[:], T.mi[:], T.cols[:, 2:3], O.add, "mi cl2", "mL")
        for i in range(16):
            ts(T.EW[:, i, :], T.mmB[:], float(i), O.is_equal, "mmB cl2", "EW%d" % i, T.cols[:, 2:3], O.mult)
            ts(T.EH[:, i, :], T.mmB[:], float(i), O.is_equal, "mmB cl3", "EH%d" % i, T.cols[:, 4:5], O.mult)
        wr["EW"] = wr["EW15"]
        wr["EH"] = wr["EH15"]
        ts(T.Dm[:], T.mL[:], float(LN - 129), O.add, "mL", "Dm")
        ts(sm(9), T.mL[:, 0:16], float(4096 - 129 - 2047), O.add, "mL", "bz")
        ts(sm(10), sm(9), 2047.0, O.add, "bz", "bz16", 16.0, O.mult)
        for i in range(16):
            act(T.D15[:, i, :], T.B15[:], AF.Copy, "B15 RSn", "D15%d" % i, scale=T.RSn[:, i:i + 1])
        wr["D15"] = wr["D1515"]

    TCR = "TC TC_0 TC_1 TC_2 TC_3 TCz"
    TSR = "TS TS_0 TS_1 TS_2 TS_3 TSz TSF TSF0 TSF1"
    TLR = "TL TLa TLb"
    Wt = [W0]
    PX, PL = (T.PX0, T.PX1), (T.PL0, T.PL1)

    def K(s, h):
        return s.replace("@", str(h))

    def HL(h):
        return slice(1024 * h, 1024 * h + 1024)

    def HC(h):
        return slice(64 * h, 64 * h + 64)

    def S1(h, t, s):
        win = T.TC[:, 0:Wt[0]].indirect(cu[:, HC(h)])
        if t == 0 and s == 0:
            cp(T.q[:, HL(h)], win, TCR + K(" cu@", h), K("q@", h))
        else:
            tt(T.q[:, HL(h)], win, T.mk[:, HL(h)], O.mult, TCR + K(" cu@ mk@", h), K("q@", h))

    def S2(h):
        act(T.G[:, HL(h)], T.q[:, HL(h)], AF.Sigmoid, K("q@", h), K("G@", h), bias=-200.0, scale=400.0)

    def S3q(h):
        listsum(PL[h][:, 0:64], T.ES, T.q, 1024 * h, 1024 * h + 1024, K("q@ ES", h), K("PL@", h))
        listsum(PL[h][:, 64:128], T.ES, T.q, 1024 * h, 1024 * h + 1024, K("q@ ES", h), K("PL@", h), stop=False)

    def S3G(h):
        listsum(PL[h][:, 64:128], T.ES, T.G, 1024 * h, 1024 * h + 1024, K("G@ ES", h), K("PL@", h), start=False)

    def S3p(h):
        def f():
            for b in (0, 512):
                x = P.matmul(PX[h][:, b:b + 512], T.PRE[:], T.q[:, 1024 * h + b:1024 * h + b + 512], True, False)
            return x
        p_(f, K("q@ PRE", h), K("PX@0 PX@1", h))

    def S4(h, s, o=None):
        C = HC(h)
        fill = [] if o is None else S11(o)
        tt(T.xx[:, C], PL[h][:, 64:128], T.vl[:, 128 * s + 64 * h:128 * s + 64 * h + 64], O.mult, K("PL@ vl", h), K("xx@", h))
        tt(T.es[:, C], PL[h][:, 0:64], T.xx[:, C], O.is_le, K("PL@ xx@", h), K("es@", h))
        for f in fill[0:1]:
            f()
        tt(T.es[:, C], T.es[:, C], nz[:, C], O.mult, K("es@ nz@", h), K("es@", h))
        for f in fill[1:2]:
            f()
        tt(T.c2f[:, C], cf[:, C], T.es[:, C], O.add, K("cf@ es@", h), K("c2f@", h))
        tt(T.x2[:, C], T.xx[:, C], T.es[:, C], O.add, K("xx@ es@", h), K("x2@", h))
        cp(T.cu2[:, C], T.c2f[:, C], K("c2f@", h), K("cu2@", h))
        for f in fill[2:3]:
            f()
        ts(T.th[:, C], T.x2[:, C], 1025.0 - 0.4975, O.add, K("x2@", h), K("th@", h))

    def flist(s):
        ts(sm(5), T.es[:, 0:16], 0.5, O.is_gt, "es0", "e01")
        ts(sm(1), cf[:, 0:16], 1.0, O.add, "cf0", "d1")
        ts(sm(2), sm(0), 0.5, O.is_lt, "F1", "t1")
        tt(sm(3), sm(2), sm(1), O.mult, "t1 d1", "t2")
        tt(sm(4), sm(0), sm(3), O.add, "F1 t2", "Fo")
        if s == SP - 1:
            tt(sm(2), sm(0), sm(5), O.is_gt, "F1 e01", "t1")
            tt(sm(6), sm(2), sm(5), O.subtract, "t1 e01", "t2")
            ts(sm(6), sm(6), 0.5, O.is_gt, "t2", "ca t2")
            ts(T.kh[:, 32:48], sm(6), -1.0, O.mult, "ca", "kh2")
        tt(sm(0), sm(4), sm(5), O.mult, "Fo e01", "F1")
        if s == SP - 2:
            ts(sm(7), sm(0), -2048.0, O.add, "F1", "kf")
            ts(T.kh[:, 0:16], sm(7), -1.0, O.mult, "kf", "kh0")

    def S5(h):
        act(T.Sg[:, HL(h)], T.TS[:, 0:TW + Wt[0]].indirect(T.cu2[:, HC(h)]), AF.Copy, TSR + K(" cu2@", h), K("Sg@", h))

    def P6(h):
        for b in (0, 1):
            spread(PX[h], 512 * b, 512, T.Dn, T.th, 64 * h + 32 * b, K("th@ Dn", h), K("PX@%d" % b, h), start=False)

    def S7(h):
        for b in (0, 1):
            act(T.cm[:, 1024 * h + 512 * b:1024 * h + 512 * b + 512], PX[h][:, 512 * b:512 * b + 512], AF.Sigmoid, K("PX@%d cl0 cl1" % b, h),
                K("cm@%d" % b, h), bias=T.cols[:, 1:2], scale=T.cols[:, 0:1])

    def P8(h, ps, lhs, r, w):
        for b in (0, 1):
            p_(lambda: P.matmul(ps[:, 512 * b:512 * b + 512], lhs[:], T.cm[:, 1024 * h + 512 * b:1024 * h + 512 * b + 512], True, True),
               K(r % b, h), K(w % b, h))

    def P8u(h):
        P8(h, T.PU, T.DL, "cm@%d DL", "PU%d")

    def P8t(h):
        P8(h, PX[h], T.BN, "cm@%d BN", "PX@%d")

    def S9(h, s):
        tt(T.Y[:, HL(h)], T.Sg[:, HL(h)], T.PU[:], O.mult, K("Sg@ PU0 PU1", h), K("Y@", h))
        if s == SP - 1 and h == 0:
            act(T.uf[:], T.PU[:, 0:256], AF.Copy, "PU0", "uf")

    def S10(h):
        listsum(PL[h][:, 128:192], T.ES, T.Y, 1024 * h, 1024 * h + 1024, K("Y@ ES", h), K("PL@", h))

    def M(h):
        tt(T.mk[:, HL(h)], T.q[:, HL(h)], PX[h][:], O.is_lt, K("q@ PX@0 PX@1", h), K("mk@", h))

    def S11(h):
        C, y = HC(h), PL[h][:, 128:192]
        return [lambda: ts(cu[:, C], y, 2048.0, O.add, K("PL@", h), K("cu@", h)),
                lambda: ts(cf[:, C], y, 2048.0, O.add, K("PL@", h), K("cf@", h)),
                lambda: ts(nz[:, C], y, -2047.5, O.is_gt, K("PL@", h), K("nz@", h), float(TW), O.mult)]

    def eqs(x):
        def one(k):
            return lambda: ts(T["EQ%d" % x][:, k, 0:256 - 16 * k], T.R[:, 256 * x + 16 * k:256 * x + 256], T.sm[:, 112 + 16 * x + k:113 + 16 * x + k],
                              O.is_equal, "R%d %s" % (x, ("kf", "kd")[x]), "E%d_%d" % (x, k))
        alle = " ".join("E%d_%d" % (x, k) for k in range(16))
        d = T["EQ%d" % x][:, :, 0:16]
        return [one(k) for k in range(16)] + [lambda: tt(d, d, T.tri[:], O.mult, alle + " tri", alle)]

    def rows(c, kn, ps, base, key):
        spread(ps, base, 256, T.Dn, T.kh, c, "Dn " + kn, key)

    def slot(h, t, s, o, so):
        keyf, keyd, cand = h == 1 and s == SP - 2, h == 0 and s == SP - 1, h == 1 and s == SP - 1
        eq = eqs(0)[0:9] if keyd else eqs(0)[9:] if cand else []
        S1(h, t, s)
        if o is not None:
            P8u(o)
        S2(h)
        S3q(h)
        if keyd:
            ts(sm(8), cf[:, 0:16], 1.0 - 2048.0, O.add, "cf0", "kd")
            ts(T.kh[:, 16:32], sm(8), -1.0, O.mult, "kd", "kh1")
        for f in eq[0:2]:
            f()
        if o is not None:
            S9(o, so)
        if h == 1:
            flist(s)
        else:
            for f in eq[2:]:
                f()
        S3G(h)
        if o is not None:
            S10(o)
            if marks(t, so):
                P8t(o)
        S3p(h)
        if keyf:
            rows(0, "kh0", T.PU, 0, "PU0")
        if keyd:
            rows(16, "kh1", T.PU, 0, "PU0")
        if t == s == 0 and h == 0:
            tables2()
        S4(h, s, o)
        P6(h)
        if cand:
            rows(32, "kh2", T.PL0, 256, "PL0")
        S5(h)
        if cand:
            act(T.cr[:], T.PL0[:, 256:512], AF.Copy, "PL0", "cr")
        if t == s == 0 and h == 0:
            consts2()
        if keyf:
            cp(T.R[:, 0:256], T.PU[:, 0:256], "PU0", "R0")
        if keyd:
            cp(T.R[:, 256:512], T.PU[:, 0:256], "PU0", "R1")
        if o is not None and marks(t, so):
            M(o)
        S7(h)
        if cand:
            for f in eq[2:]:
                f()
            for k in range(16):
                act(T.BC[:, k, :], T.BO[:], AF.Copy, "BO ca", "BC%d" % k, scale=T.sm[:, 96 + k:97 + k])

    def dups(x):
        def f():
            for k in range(16):
                y = P.matmul(PL[x][:, 256 + 16 * k:512], T.BC[:, k, :], T["EQ%d" % x][:, k, 0:256 - 16 * k], k == 0, k == 15)
            return y
        p_(f, " ".join("E%d_%d BC%d" % (x, k, k) for k in range(16)), "PL%d" % x)

    def firsts(x):
        sl = slice(256 * x, 256 * x + 256)
        tt(T.fr[:, sl], PL[x][:, 256:512], T.cr[:], O.is_lt, "PL%d cr" % x, "fr%d" % x)
        listsum(PL[x][:, 192:208], T.ES, T.fr, 256 * x, 256 * x + 256, "fr%d ES" % x, "PL%d" % x)

    def offs(x):
        kk, o, kn = 7 + x, slice(16 * x, 16 * x + 16), ("kf", "kd")[x]
        tt(T.o1[:, o], sm(kk), sm(9), O.subtract, kn + " bz", "o1%d" % x)
        tt(T.o2[:, o], T.o1[:, o], PL[x][:, 192:208], O.mult, "o1%d PL%d" % (x, x), "o2%d" % x)
        tt(T.o1[:, o], T.o2[:, o], sm(10), O.add, "o2%d bz16" % x, "o1%d" % x)
        ts(T.ou[:, o], T.o1[:, o], 1.0 / 16, O.mult, "o1%d" % x, "ou%d" % x)

    for t in range(RO):
        last = t == RO - 1
        iota(T.MK[:], [[0, 640]], 0, 0, "MK")
        iota(T.H[:, 0:LN], [[0, LN]], 0, 0, "H")
        for s in range(SP):
            slot(0, t, s, 1 if s else None, s - 1)
            slot(1, t, s, 0, s)
            if t == s == 0:
                late()
        if not last:
            loadv("S", t + 1)
        tot = T.PX0[:, 0:128]
        ts(T.eb[:], T.es[:], 0.5, O.is_gt, "es0 es1", "eb")
        p_(lambda: P.matmul(tot, T.BO[:], T.eb[:], True, True), "BO eb", "PX00")
        p_(lambda: P.matmul(T.PX0[:, 512:640], T.ZT[:], T.eb[:], True, True), "ZT eb", "PX01")
        v_(lambda: V.tensor_tensor_scan(T.inc[:], tot, T.zz[:], 128.0, O.add, O.add), "PX00 zz", "inc")
        ts(T.hc[:], tot, 0.5, O.is_gt, "PX00", "hc")
        tt(T.ha[:], T.inc[:], tot, O.subtract, "inc PX00", "ha")
        tt(T.X[:], T.inc[:], T.PX0[:, 512:640], O.add, "inc PX01", "X")
        ts(T.hb[:], T.ha[:], 639.5, O.is_lt, "ha", "hb")
        tt(T.ha[:], T.ha[:], T.hc[:], O.mult, "ha hc", "ha")
        tt(T.ha[:], T.ha[:], T.hb[:], O.mult, "ha hb", "ha")
        tt(T.off[:], T.ha[:], T.krow[:], O.max, "ha krow", "off")
        listsum(T.PX0[:, 0:8], T.ES, T.off, 0, 128, "off ES", "PX00")
        P8u(1)
        if not last:
            def f():
                for b in (0, 512):
                    P.matmul(T.PX1[:, b:b + 512], T.NI[:], T.q[:, 1024 + b:1536 + b], True, False)
                    x = P.matmul(T.PX1[:, b:b + 512], T.BN[:], T.cm[:, 1024 + b:1536 + b], False, True)
                return x
            p_(f, "q1 cm10 cm11 NI BN", "PX10 PX11")
        ts(T.tot[:, 0:1], T.inc[:, 127:128], -128.0, O.add, "inc", "tot")
        send(T["lT%d" % t][:, 0:1], T.tot[:, 0:1], "T", t, "tot")
        tt(T.X[:], T.X[:], T.eb[:], O.mult, "X eb", "X")
        eq = eqs(1)
        for f in eq[0:4]:
            f()
        ts(T.ofu[:], T.PX0[:, 0:8], 1.0 / 16, O.mult, "PX00", "ofu")
        cp(T.MK[:, 0:640].indirect(T.ofu[:]), T.krow[:], "krow ofu", "MK")
        for f in eq[4:6]:
            f()
        v_(lambda: V.tensor_tensor_scan(T.kr[:], T.MK[:, 128:640], T.MK[:, 128:640], 0.0, O.max, O.max), "MK", "kr")
        S9(1, SP - 1)
        S10(1)
        listsum(T.PX0[:, 0:32], T.ES, T.kr, 0, 512, "kr ES", "PX00")
        dups(0)
        for f in eq[6:12]:
            f()
        if not last:
            act(T.mk[:, HL(1)], T.PX1[:], AF.Sigmoid, "PX10 PX11", "mk1", bias=-200.0, scale=400.0 / D)
        act(T.nu[:], T.uf[:], AF.Identity, "uf", "nu", bias=1.0, scale=-1.0)
        act(T.u1[:], T.uf[:], AF.Copy, "uf", "u1", scale=1.0 - D)
        for f in S11(1):
            f()
        ts(T.klu[:], T.PX0[:, 0:32], 1.0 / 16, O.mult, "PX00", "klu")
        ts(T.Yl[:], cf[:], -2048.0, O.add, "cf0 cf1", "Yl")
        tt(T.OH[:], T.X[:].indirect(T.klu[:]), T.mrow[:], O.is_equal, "X klu mrow", "OH")
        tt(T.CG[:], T.Yl[:].indirect(T.klu[:]), T.OH[:], O.mult, "Yl klu OH", "CG")
        for f in eq[12:]:
            f()
        if not last:
            listsum(T.PX0[:, 0:32], T.ES, T.kr, 0, 512, "kr ES", "PX00", stop=False)
            listsum(T.PX0[:, 0:32], T.EW, T.OH, 0, 512, "OH EW", "PX00", start=False)
            listsum(T.PX0[:, 512:544], T.ES, T.CG, 0, 512, "CG ES", "PX01")
        else:
            listsum(T.PX0[:, 512:544], T.ES, T.CG, 0, 512, "CG ES", "PX01")
            listsum(T.PX0[:, 0:32], T.ES, T.kr, 0, 512, "kr ES", "PX00", stop=False)
            listsum(T.PX0[:, 0:32], T.EW, T.OH, 0, 512, "OH EW", "PX00", start=False)
        firsts(0)
        dups(1)
        if not last:
            cp(T.lnu[:], T.PX0[:, 0:32], "PX00", "lnu")
            act(T.MS[:], T.mk[:, 0:LN].indirect(T.lnu[:]), AF.Copy, "mk0 mk1 lnu", "MS")
            send(T["lM%d" % t][:], T.MS[:], "M", t, "MS")
        ts(T.cmu[:], T.PX0[:, 512:544], 2048.0, O.add, "PX01", "cmu")
        act(T.Lg[:], T.TL[:, 0:Wt[0]].indirect(T.cmu[:]), AF.Copy, TLR + " cmu", "Lg")
        send(T["lL%d" % t][:], T.Lg[:], "L", t, "Lg")
        offs(0)
        firsts(1)
        act(T.lnf[:], T.PX0[:, 0:32], AF.Copy, "PX00", "lnf")
        wb = slice(W0 + B * t, W0 + B * (t + 1))
        wf = slice(TW + W0 + B * t, TW + W0 + B * (t + 1))
        if not last:
            act(T.TS[:, wb], T.TS[:, 0:Wt[0]].indirect(cu[:, 0:16]), AF.Copy, TSR + " cu0", "TS")
            act(T.TL[:, wb], T.TL[:, 0:Wt[0]].indirect(cu[:, 0:16]), AF.Copy, TLR + " cu0", "TL")
            ts(T.kh[:, 48:64], T.Yl[:, 0:16], -1.0, O.mult, "Yl", "kh3")
            spread(T.PU, 0, 256, T.D15, T.kh, 48, "D15 kh3", "PU0")
            act(T.TS[:, wf], T.PU[:, 0:256], AF.Copy, "PU0", "TS")
            tt(T.uw[:], T.uf[:], T["wr%d" % t][:], O.mult, "uf wr%d" % t, "uw")
        v_(lambda: V.tensor_scalar(T.rr[:], T.TC[:, 0:Wt[0]].indirect(cu[:, 0:16]), 0.5, 0.25, O.mult, O.add), TCR + " cu0", "rr")
        offs(1)
        tt(T.r2[:], T.rr[:], T.fr[:, 0:256], O.mult, "rr fr0", "r2")
        if not last:
            vlist(t + 1)
        ts(T.TC[:, wb], T.r2[:], -D, O.add, "r2", "TC")
        tt(T.aC[:], T.TC[:].indirect(T.ou[:, 0:16]), T.nu[:], O.mult, TCR + " ou0 nu", "aC")
        tt(T.TC[:].indirect(T.ou[:, 0:16]), T.aC[:], T.u1[:], O.add, "aC u1 ou0", "TC")
        if not last:
            tt(T.aS[:], T.TS[:, 0:TW].indirect(T.ou[:, 0:16]), T.nu[:], O.mult, TSR + " ou0 nu", "aS")
            tt(T.TS[:, 0:TW].indirect(T.ou[:, 0:16]), T.aS[:], T.uw[:], O.add, "aS uw ou0", "TS")
        tt(T.aC[:], T.TC[:].indirect(T.ou[:, 16:32]), T.uf[:], O.add, TCR + " ou1 uf", "aC")
        ts(T.aC[:], T.aC[:], 15.0 - D, O.min, "aC", "aC")
        cp(T.TC[:].indirect(T.ou[:, 16:32]), T.aC[:], "aC ou1", "TC")
        Wt[0] += B
        if last:
            for k in range(4):
                for b in (0, 1):
                    o = slice(1024 * k + 512 * b, 1024 * k + 512 * b + 512)
                    if b or k == 3:
                        act(T.yb[:, o], T.TC[:, o], AF.Relu, TCR, "yb%d%d" % (k, b))
                    else:
                        ts(T.yb[:, o], T.TC[:, o], 0.0, O.max, TCR, "yb%d%d" % (k, b))
                o = slice(1024 * k, 1024 * k + 1024)
                dma("S", T.yn[:, o], T.yb[:, o], "yb%d0 yb%d1" % (k, k), "yn%d" % k)
        tt(T.tot[:, 1:2], T.tot[:, 0:1], T["lT%d" % t][:, 0:1], O.min, "tot lT%d" % t, "tm1")
        tt(T.so[:], T.lnf[:], T.Dm[:], O.subtract, "lnf Dm", "so")
        ts(T.tot[:, 2:3], T.tot[:, 1:2], float(CAP), O.min, "tm1", "tm2", 128.0, O.add)
        tm = T.tot[:, 2:3]
        ts(T.vd[:], T.mL[:], tm, O.is_le, "mL tm2", "vd")
        ts(T.mvv[:], T.X[:], tm, O.is_le, "X tm2", "mvv")
        tt(T.so[:], T.so[:], T.vd[:], O.mult, "so vd", "so")
        tt(T.mvv[:], T.mvv[:], T.eb[:], O.mult, "mvv eb", "mvv")
        tt(T.so[:], T.so[:], T.Dm[:], O.add, "so Dm", "so")
        ts(T.nmv[:], T.mvv[:], -1.0, O.mult, "mvv", "nmv", 1.0, O.add)
        cp(T.sou[:], T.so[:], "so", "sou")
        tt(cf[:], cf[:], T.nmv[:], O.mult, "cf0 cf1 nmv", "cf0 cf1")
        if not last:
            tt(sm(0), sm(0), T.nmv[:, 0:16], O.mult, "F1 nmv", "F1")
        cp(T.H[:].indirect(T.sou[:]), T["lL%d" % t][:], "sou lL%d" % t, "H")
        listsum(T.PX0[:, 0:128], T.EH, T.H, 0, LN, "EH H", "PX00")
        if not last:
            cp(T.mk[:].indirect(T.sou[:]), T["lM%d" % t][:], "sou lM%d" % t, "mk0 mk1")
        tt(cf[:], cf[:], T.PX0[:, 0:128], O.add, "cf0 cf1 PX00", "cf0 cf1")
        if not last:
            cp(cu[:], cf[:], "cf0 cf1", "cu0 cu1")
            ts(nz[:], cf[:], 0.5, O.is_gt, "cf0 cf1", "nz0 nz1", float(TW), O.mult)
    dma("A", T.yc[:, :], cf[:], "cf0 cf1", "yc")
    for s in sorted(left):
        if seen["G"].get(s, 0) < left[s]:
            g.wait_ge(T.sem[s], left[s])
